import numpy as np
import ml_dtypes


def mxq(x, axis, fmt="e4m3"):
    dtype, down = {"e4m3": (ml_dtypes.float8_e4m3fn, 7), "e5m2": (ml_dtypes.float8_e5m2, 14)}[fmt]
    v = np.moveaxis(np.asarray(x, np.float32).astype(ml_dtypes.bfloat16).astype(np.float64), axis, -1)
    blocks = v.reshape(v.shape[:-1] + (-1, 32))
    amax = np.abs(blocks).max(-1, keepdims=True)
    byte = np.maximum(np.where(amax > 0, np.frexp(amax)[1] - 1 + 127, 0) - down, 1)
    scale = np.exp2(byte - 127.0)
    codes = (blocks / scale).astype(np.float32).astype(dtype).astype(np.float64)
    return np.moveaxis((codes * scale).reshape(v.shape), -1, axis)


WIDE = False


def mx_kscale(k):
    if not WIDE:
        return np.ones(k)
    levels = np.array([10, -10, 5, -5, 0])
    if k % 512:
        return np.exp2(np.random.permutation(np.resize(levels, k // 32))).repeat(32)
    a = np.empty((k // 512, 16))
    for p in range(k // 512):
        a[p, :8] = np.random.permutation(np.resize(levels, 8))
        for g in range(8):
            far = levels[np.abs(levels - a[p, g]) >= 10]
            a[p, g + 8] = far[np.random.randint(len(far))]
    return np.exp2(a.ravel()).repeat(32)


def f64(x):
    return np.asarray(x).astype(np.float64)


def striped(idx):
    return np.tile(idx.reshape(-1, 16).T, (8, 1)).astype(np.uint16)


def unstriped(offs):
    return offs[:16].T.reshape(-1).astype(np.int64)


E2M1 = np.array([0.0, 0.5, 1.0, 1.5, 2.0, 3.0, 4.0, 6.0, -0.0, -0.5, -1.0, -1.5, -2.0, -3.0, -4.0, -6.0])


def pack_weight(w, fmt):
    k, n = w.shape
    w = f64(np.asarray(w, np.float32).astype(ml_dtypes.bfloat16)).reshape(k // 32, 32, n)
    amax = np.abs(w).max(1)
    if fmt == "e4m3":
        byte = np.frexp(amax)[1] - 1 + 127 - 7
    else:
        mant, ex = np.frexp(amax / 6.0)
        byte = np.where(mant > 0.5, ex, ex - 1) + 127
    byte = np.clip(np.where(amax > 0, byte, 1), 1, 254)
    scaled = (w * np.exp2(127.0 - byte)[:, None, :]).reshape(k, n).astype(np.float32)
    by_word = np.ascontiguousarray(scaled.reshape(k // 512, 128, 4, n).transpose(0, 1, 3, 2))
    if fmt == "e4m3":
        words = by_word.astype(ml_dtypes.float8_e4m3fn).view(np.uint8)
    else:
        c = by_word.astype(ml_dtypes.float4_e2m1fn).view(np.uint8) & 0xF
        words = (c[..., 0::2] | (c[..., 1::2] << 4)).reshape(k // 512, 128, 2 * n)
    return np.ascontiguousarray(words), np.ascontiguousarray(byte.astype(np.uint8).reshape(k // 512, 16, n))


def unpack_weight(words, scales, fmt):
    g, _, n = scales.shape
    words = np.ascontiguousarray(words).reshape(g, 128, n, -1)
    if fmt == "e4m3":
        vals = words.view(ml_dtypes.float8_e4m3fn).astype(np.float64)
    else:
        nib = np.empty((g, 128, n, 4), np.uint8)
        nib[..., 0::2] = words & 0xF
        nib[..., 1::2] = words >> 4
        vals = E2M1[nib]
    vals = vals * np.repeat(np.exp2(scales.astype(np.float64) - 127.0), 8, axis=1)[..., None]
    return vals.transpose(0, 1, 3, 2).reshape(g * 512, n)


def gelu(v):
    return 0.5 * v * (1.0 + np.tanh(np.sqrt(2.0 / np.pi) * (v + 0.044715 * v**3)))


K, H, N, T, S = 1024, 512, 256, 2048, 1024

def setup_inputs():
    n = np.random.standard_normal
    s = mx_kscale(K)[:, None]
    u = mx_kscale(H)[:, None]
    tab_words, tab_scales = pack_weight(n((K, T)) * s, "e4m3")
    wh = (n((K, H)) * 0.6 / np.sqrt(K) / s).astype(np.float32)
    wr_words, wr_scales = pack_weight(n((K, H)) * 0.6 / np.sqrt(K) / s, "e2m1")
    wt_words, wt_scales = pack_weight(n((K, H)) * 0.6 / np.sqrt(K) / s, "e4m3")
    g = (np.exp(0.3 * n(H)) * u[:, 0]).astype(np.float32)
    wo = (n((H, N)) * 2.0 / np.sqrt(H) / u).astype(np.float32)
    b = (0.5 * n(N)).astype(np.float32)
    return dict(tab_words=tab_words, tab_scales=tab_scales,
                offs=striped(np.random.permutation(T)[:S]),
                offs2=striped(np.random.permutation(T)[:S]),
                offs3=striped(np.random.permutation(T)[:S]),
                wh=wh, wr_words=wr_words, wr_scales=wr_scales,
                wt_words=wt_words, wt_scales=wt_scales, g=g, wo=wo, b=b)

def reference(tab_words, tab_scales, offs, offs2, offs3, wh, wr_words, wr_scales, wt_words, wt_scales, g, wo, b):
    v = unpack_weight(tab_words, tab_scales, "e4m3")
    vh, vr, vt = v[:, unstriped(offs)], v[:, unstriped(offs2)], v[:, unstriped(offs3)]
    wr = unpack_weight(wr_words, wr_scales, "e2m1")
    wt = unpack_weight(wt_words, wt_scales, "e4m3")
    a = mxq(f64(wh), 0, "e4m3").T @ vh + wr.T @ vr
    t = wt.T @ vt
    h = np.exp(-np.abs(a - t)) * f64(g)[:, None]
    y = mxq(f64(wo), 0, "e4m3").T @ mxq(h, 0, "e4m3")
    return y + f64(b)[:, None]

@@ -1,0 +1,295 @@
+from contextlib import ExitStack
+
+import concourse.mybir as mybir
+
+K, H, N, T, S = 1024, 512, 256, 2048, 1024
+FLOPS = 2 * (3 * K * H * S + H * N * S)
+
+F32 = mybir.dt.float32
+BF16 = mybir.dt.bfloat16
+I32 = mybir.dt.int32
+U32 = mybir.dt.uint32
+U16 = mybir.dt.uint16
+U8 = mybir.dt.uint8
+E4M3 = mybir.dt.float8_e4m3fn_x4
+E2M1 = mybir.dt.float4_e2m1fn_x4
+ACT = mybir.ActivationFunctionType
+ALU = mybir.AluOpType
+
+P = 128
+PACK = 4
+RUN = 8
+PASSES = K // (P * PACK)
+CHUNK = 256
+TILES = S // P
+GROUPS = [(0, 1), (2, 3), (4, 5), (6,), (7,)]
+GAIN_ON_GPSIMD = ()
+BIAS_ON_VECTOR = ()
+
+
+def tile_list_triple_plausibility_readout_kernel(
+    tc, tab_words, tab_scales, offs, offs2, offs3, wh, wr_words, wr_scales, wt_words, wt_scales, g, wo, b, out
+):
+    nc = tc.nc
+    with ExitStack() as ctx:
+        keep = ctx.enter_context(tc.tile_pool(name="keep", bufs=1))
+        ring = ctx.enter_context(tc.tile_pool(name="ring", bufs=2))
+        psum = ctx.enter_context(tc.psum_pool(name="psum", bufs=2))
+
+        lists, picked_sc, picked, wh_raw, wh_w, wh_sc, tab = {}, {}, {}, {}, {}, {}, {}
+        t_sb, diff, match, h_q = {}, {}, {}, {}
+        tab_sc = keep.tile([P, T], U8, name="tab_sc", align_bytes=64)
+        w_sc_raw = keep.tile([P, 2, PASSES, H], U8, name="w_sc_raw", align_bytes=64)
+        w_sc = keep.tile([P, 2, PASSES, PACK, P], U8, name="w_sc", align_bytes=64)
+        rel_sc1 = keep.tile([P, S], U8, name="rel_sc1", align_bytes=64)
+        warm = keep.tile([P, 2], F32, name="warm")
+        wo_raw = keep.tile([P, PACK, N], F32, name="wo_raw")
+        wt_raw = keep.tile([P, PASSES, H], I32, name="wt_raw", align_bytes=64)
+        wt_w = keep.tile([P, PASSES, PACK, P], I32, name="wt_w", align_bytes=64)
+        wr_raw = keep.tile([P, PASSES, H // 2], I32, name="wr_raw", align_bytes=64)
+        wr_w = keep.tile([P, PASSES, PACK, 2 * P], U8, name="wr_w", align_bytes=64)
+        gain = keep.tile([P, PACK], F32, name="gain")
+        bias = keep.tile([P, 2], F32, name="bias")
+        wo_bf = keep.tile([P, 2, P, PACK], BF16, name="wo_bf", align_bytes=64)
+        wo_w = keep.tile([P, N], U32, name="wo_w", align_bytes=64)
+        wo_sc = keep.tile([P, N], U8, name="wo_sc", align_bytes=64)
+        out_v = out.rearrange("(p c) j -> p c j", c=2)
+
+        def load_list(name):
+            lists[name] = keep.tile([P, S // 16], U16, name="list_" + name)
+            nc.sync.dma_start(lists[name][:], {"head": offs, "rel": offs2, "tail": offs3}[name])
+
+        def load_tab_scales():
+            for q in range(4):
+                nc.sync.dma_start(
+                    out=tab_sc[32 * q : 32 * q + 8, :].bitcast(I32),
+                    in_=tab_scales[:, 4 * q : 4 * q + 4, :].bitcast(I32),
+                )
+
+        def load_weight_scales(engine, w, quadrants=range(4)):
+            for q in quadrants:
+                engine.dma_start(
+                    out=w_sc_raw[32 * q : 32 * q + 4, w, :, :].bitcast(I32),
+                    in_=(wt_scales, wr_scales)[w][:, 4 * q : 4 * q + 4, :].rearrange("a r c -> r a c").bitcast(I32),
+                )
+
+        def load_tab_pass(a):
+            words = keep.tile([P, T], I32, name="tab%d" % a, align_bytes=64)
+            nc.sync.dma_start(out=words[:], in_=tab_words[a].rearrange("p t i -> p (t i)").bitcast(I32))
+            tab[a] = words[:]
+
+        def load_tab():
+            words = keep.tile([P, PASSES, T], I32, name="tab", align_bytes=64)
+            nc.sync.dma_start(out=words[:], in_=tab_words.rearrange("a p t i -> p a (t i)").bitcast(I32))
+            for a in range(PASSES):
+                tab[a] = words[:, a, :]
+
+        def load_wh(a):
+            wh_raw[a] = keep.tile([P, PACK, H], F32, name="wh_raw%d" % a)
+            nc.sync.dma_start(out=wh_raw[a][:], in_=wh[512 * a : 512 * (a + 1), :].rearrange("(p i) c -> p i c", i=PACK))
+
+        def load_wt():
+            nc.sync.dma_start(out=wt_raw[:], in_=wt_words.rearrange("a p c i -> p a (c i)").bitcast(I32))
+
+        def load_wr():
+            nc.sync.dma_start(out=wr_raw[:], in_=wr_words.rearrange("a p c -> p a c").bitcast(I32))
+
+        def load_wo():
+            rows = wo.rearrange("(q s e) n -> s q e n", s=PACK, e=RUN)
+            for s in range(PACK):
+                nc.sync.dma_start(out=wo_raw[:, s, :], in_=rows[s])
+
+        def load_vectors():
+            gain_raw = keep.tile([P, PACK, RUN], F32, name="gain_raw")
+            values = g.rearrange("(q s e o) -> s q e o", s=PACK, e=RUN, o=1)
+            with nc.allow_non_contiguous_dma(reason="one gain value for each partition"):
+                for s in range(PACK):
+                    nc.sync.dma_start(out=gain_raw[:, s, 0:1], in_=values[s])
+            nc.scalar.copy(out=gain[:], in_=gain_raw[:, :, 0])
+            nc.sync.dma_start(out=bias[:], in_=b.rearrange("(p c) -> p c", c=2))
+
+        def gather_scales(name, lo=0, hi=S):
+            if lo == 0:
+                picked_sc[name] = keep.tile([P, S], U8, name="sc_" + name, align_bytes=64)
+            nc.vector.tensor_copy(out=picked_sc[name][:, lo:hi], in_=tab_sc[:].indirect(lists[name][:, lo // 16 : hi // 16]))
+
+        def lower_rel_scales(engine):
+            engine.dma_start(out=rel_sc1[0:100, :].bitcast(I32), in_=picked_sc["rel"][4:104, :].bitcast(I32))
+
+        def order_scales(engine):
+            engine.tensor_copy(
+                out=w_sc[:].bitcast(I32).rearrange("p w a s (q e) -> p (w a) s q e", e=RUN // 4),
+                in_=w_sc_raw[:].bitcast(I32).rearrange("p w a (q s e) -> p (w a) s q e", s=PACK, e=RUN // 4),
+            )
+
+        def order_wt(engine):
+            engine.tensor_copy(
+                out=wt_w[:].rearrange("p a s (q e) -> p a s q e", e=RUN),
+                in_=wt_raw[:].rearrange("p a (q s e) -> p a s q e", s=PACK, e=RUN),
+            )
+
+        def order_wr(engine):
+            engine.tensor_copy(
+                out=wr_w[:].bitcast(I32).rearrange("p a s (q e) -> p a s q e", e=RUN // 2),
+                in_=wr_raw[:].rearrange("p a (q s e) -> p a s q e", s=PACK, e=RUN // 2),
+            )
+
+        def quantise_wh(a):
+            woven = ring.tile([P, PACK, P, PACK], BF16, name="wh_bf", tag="wh_bf%d" % a, bufs=1, align_bytes=64)
+            wh_w[a] = keep.tile([P, PACK, P], U32, name="wh_w%d" % a, align_bytes=64)
+            wh_sc[a] = keep.tile([P, PACK, P], U8, name="wh_sc%d" % a, align_bytes=64)
+            nc.scalar.copy(
+                out=woven[:].rearrange("p s (q e) i -> p s q e i", e=RUN),
+                in_=wh_raw[a][:].rearrange("p i (q s e) -> p s q e i", s=PACK, e=RUN),
+            )
+            nc.vector.quantize_mx(
+                out=wh_w[a][:].rearrange("p s m -> p (s m)").bitcast(E4M3),
+                scales=wh_sc[a][:].rearrange("p s m -> p (s m)"),
+                in_=woven[:].rearrange("p s m i -> p (s m i)"),
+            )
+
+        def quantise_wo():
+            nc.scalar.copy(out=wo_bf[:], in_=wo_raw[:].rearrange("p i (m c) -> p c m i", c=2))
+            nc.vector.quantize_mx(out=wo_w[:].bitcast(E4M3), scales=wo_sc[:], in_=wo_bf[:].rearrange("p c m i -> p (c m i)"))
+
+        def gather_words(names, chunk, tag, bufs=1):
+            cols = slice(chunk * CHUNK // 16, (chunk + 1) * CHUNK // 16)
+            got = ring.tile([P, len(names), PASSES, CHUNK], U32, name="picked", tag=tag, bufs=bufs, align_bytes=64)
+            for x, name in enumerate(names):
+                for a in range(PASSES):
+                    nc.vector.tensor_copy(out=got[:, x, a, :], in_=tab[a].bitcast(U32).indirect(lists[name][:, cols]))
+                    picked[name, a, chunk] = got[:, x, a, :]
+
+        def moving(name, a, u):
+            near = (u * P) % CHUNK
+            return picked[name, a, u * P // CHUNK][:, near : near + P].bitcast(E4M3)
+
+        def project_tail(u):
+            far = slice(u * P, (u + 1) * P)
+            t_ps = psum.tile([P, PACK, P], F32, name="t_ps", bufs=3)
+            for a in range(PASSES):
+                for s in range(PACK):
+                    nc.tensor.matmul_mx(
+                        out=t_ps[:, s, :], lhsT=wt_w[:, a, s, :].bitcast(E4M3), lhsT_scale=w_sc[:, 0, a, s, :],
+                        rhs=moving("tail", a, u), rhs_scale=picked_sc["tail"][4 * a :, far],
+                        start=(a == 0 and s == 0), stop=(a == PASSES - 1 and s == PACK - 1),
+                    )
+            t_sb[u] = ring.tile([P, P, PACK], F32, name="t_sb", tag="t_sb%d" % u, bufs=1, align_bytes=64)
+            nc.scalar.copy(out=t_sb[u][:], in_=t_ps[:].rearrange("p s j -> p j s"))
+
+        def project_head(u):
+            far = slice(u * P, (u + 1) * P)
+            a_ps = psum.tile([P, PACK, P], F32, name="a_ps", bufs=3)
+            for a in range(PASSES):
+                for s in range(PACK):
+                    nc.tensor.matmul_mx(
+                        out=a_ps[:, s, :], lhsT=wr_w[:, a, s, :].bitcast(E2M1), lhsT_scale=w_sc[:, 1, a, s, :],
+                        rhs=moving("rel", a, u), rhs_scale=(picked_sc["rel"], rel_sc1)[a][:, far],
+                        start=(a == 0 and s == 0), stop=False,
+                    )
+            for a in range(PASSES):
+                for s in range(PACK):
+                    nc.tensor.matmul_mx(
+                        out=a_ps[:, s, :], lhsT=wh_w[a][:, s, :].bitcast(E4M3), lhsT_scale=wh_sc[a][:, s, :],
+                        rhs=moving("head", a, u), rhs_scale=picked_sc["head"][4 * a :, far],
+                        start=False, stop=(a == PASSES - 1 and s == PACK - 1),
+                    )
+            group = [gr for gr in GROUPS if u in gr][0]
+            n = len(group) * P
+            if u == group[0]:
+                diff[group] = ring.tile([P, n, PACK], F32, name="diff", bufs=5)
+            at = (u - group[0]) * P
+            nc.vector.tensor_tensor(out=diff[group][:, at : at + P, :], in0=a_ps[:].rearrange("p s j -> p j s"), in1=t_sb[u][:], op=ALU.subtract)
+            if u == group[-1]:
+                dist = ring.tile([P, n, PACK], F32, name="dist", bufs=3)
+                nc.scalar.activation(out=dist[:], in_=diff[group][:], func=ACT.Abs)
+                match[group] = ring.tile([P, n, PACK], F32, name="match", tag="match%d" % group[0], bufs=1, align_bytes=64)
+                nc.scalar.activation(out=match[group][:], in_=dist[:], func=ACT.Exp, scale=-1.0)
+
+        def weigh(group, tag="h_bf", bufs=2):
+            n = len(group) * P
+            h_bf = ring.tile([P, n, PACK], BF16, name="h_bf", tag=tag, bufs=bufs, align_bytes=64)
+            engine = nc.gpsimd if group[0] in GAIN_ON_GPSIMD else nc.vector
+            engine.tensor_tensor(out=h_bf[:], in0=match[group][:], in1=gain[:].unsqueeze(1).to_broadcast([P, n, PACK]), op=ALU.mult)
+            h_w = ring.tile([P, n], U32, name="h_w", align_bytes=64)
+            h_sc = ring.tile([P, n], U8, name="h_sc", align_bytes=64)
+            nc.vector.quantize_mx(out=h_w[:].bitcast(E4M3), scales=h_sc[:], in_=h_bf[:].rearrange("p j i -> p (j i)"))
+            h_q[group] = (h_w, h_sc)
+
+        def readout(group):
+            n = len(group) * P
+            h_w, h_sc = h_q[group]
+            y_ps = psum.tile([P, 2, n], F32, name="y_ps", bufs=2)
+            for c in range(2):
+                nc.tensor.matmul_mx(
+                    out=y_ps[:, c, :], lhsT=wo_w[:, c * P : (c + 1) * P].bitcast(E4M3),
+                    lhsT_scale=wo_sc[:, c * P : (c + 1) * P],
+                    rhs=h_w[:].bitcast(E4M3), rhs_scale=h_sc[:], start=True, stop=True,
+                )
+            y_sb = ring.tile([P, 2, n], F32, name="y_sb", bufs=5)
+            if group[0] in BIAS_ON_VECTOR:
+                nc.vector.tensor_tensor(out=y_sb[:], in0=y_ps[:], in1=bias[:].unsqueeze(2).to_broadcast([P, 2, n]), op=ALU.add)
+            else:
+                for c in range(2):
+                    nc.scalar.activation(out=y_sb[:, c, :], in_=y_ps[:, c, :], func=ACT.Identity, bias=bias[:, c : c + 1])
+            nc.sync.dma_start(out=out_v[:, :, group[0] * P : group[0] * P + n], in_=y_sb[:])
+
+        nc.vector.memset(tab_sc[:].bitcast(I32), 0)
+        nc.vector.memset(warm[:, 0:1], 0.0)
+        nc.scalar.activation(out=warm[:, 1:2], in_=warm[:, 0:1], func=ACT.Exp)
+        nc.vector.memset(w_sc_raw[:].bitcast(I32), 0)
+        nc.vector.memset(rel_sc1[:].bitcast(I32), 0)
+        load_list("rel")
+        load_tab_scales()
+        load_list("tail")
+        load_list("head")
+        load_wh(0)
+        load_weight_scales(nc.sync, 0)
+        load_wh(1)
+        load_weight_scales(nc.sync, 1)
+        load_wt()
+        load_wr()
+        load_tab_pass(0)
+        load_tab_pass(1)
+        gather_scales("rel")
+        lower_rel_scales(nc.sync)
+        load_wo()
+        load_vectors()
+        gather_scales("tail")
+        gather_scales("head")
+        quantise_wh(0)
+        quantise_wh(1)
+        order_scales(nc.vector)
+        order_wt(nc.vector)
+        order_wr(nc.vector)
+        NAMES = ["tail", "rel", "head"]
+        gather_words(NAMES, 0, "early0")
+        gather_words(NAMES, 1, "early1")
+        project_tail(0)
+        project_tail(1)
+        project_head(0)
+        project_head(1)
+        quantise_wo()
+        project_tail(2)
+        project_tail(3)
+        gather_words(NAMES, 2, "t_sb1")
+        project_head(2)
+        project_head(3)
+        project_tail(4)
+        project_tail(5)
+        weigh(GROUPS[0])
+        project_head(4)
+        project_head(5)
+        gather_words(NAMES, 3, "t_sb5")
+        readout(GROUPS[0])
+        weigh(GROUPS[1])
+        project_tail(6)
+        project_tail(7)
+        project_head(6)
+        project_head(7)
+        readout(GROUPS[1])
+        weigh(GROUPS[2], "t_sb7", 1)
+        weigh(GROUPS[3])
+        weigh(GROUPS[4])
+        for group in GROUPS[2:]:
+            readout(group)

@@ -1,6 +1,7 @@
 from contextlib import ExitStack
 
 import concourse.mybir as mybir
+from concourse.masks import make_identity
 
 K, H, N, T, S = 1024, 512, 256, 2048, 1024
 FLOPS = 2 * (3 * K * H * S + H * N * S)
@@ -18,13 +19,13 @@ ALU = mybir.AluOpType
 
 P = 128
 PACK = 4
-RUN = 8
 PASSES = K // (P * PACK)
 CHUNK = 256
 TILES = S // P
 GROUPS = [(0, 1), (2, 3), (4, 5), (6,), (7,)]
+SUB_ON_VECTOR = (6,7)
 GAIN_ON_GPSIMD = ()
-BIAS_ON_VECTOR = ()
+BIAS_ON_SCALAR = (2,4,6,7)
 
 
 def tile_list_triple_plausibility_readout_kernel(
@@ -36,18 +37,17 @@ def tile_list_triple_plausibility_readout_kernel(
         ring = ctx.enter_context(tc.tile_pool(name="ring", bufs=2))
         psum = ctx.enter_context(tc.psum_pool(name="psum", bufs=2))
 
-        lists, picked_sc, picked, wh_raw, wh_w, wh_sc, tab = {}, {}, {}, {}, {}, {}, {}
-        t_sb, diff, match, h_q = {}, {}, {}, {}
+        lists, picked_sc, picked, wh_raw, wh_bf, wh_w, wh_sc, tab = {}, {}, {}, {}, {}, {}, {}, {}
+        neg_t, pos_a, dist, match, h_q = {}, {}, {}, {}, {}
         tab_sc = keep.tile([P, T], U8, name="tab_sc", align_bytes=64)
-        w_sc_raw = keep.tile([P, 2, PASSES, H], U8, name="w_sc_raw", align_bytes=64)
-        w_sc = keep.tile([P, 2, PASSES, PACK, P], U8, name="w_sc", align_bytes=64)
+        wt_sc = keep.tile([P, PASSES, H], U8, name="wt_sc", align_bytes=64)
+        wr_sc = keep.tile([P, PASSES, H], U8, name="wr_sc", align_bytes=64)
         rel_sc1 = keep.tile([P, S], U8, name="rel_sc1", align_bytes=64)
         warm = keep.tile([P, 2], F32, name="warm")
+        ident = keep.tile([P, P], F32, name="ident")
         wo_raw = keep.tile([P, PACK, N], F32, name="wo_raw")
-        wt_raw = keep.tile([P, PASSES, H], I32, name="wt_raw", align_bytes=64)
-        wt_w = keep.tile([P, PASSES, PACK, P], I32, name="wt_w", align_bytes=64)
-        wr_raw = keep.tile([P, PASSES, H // 2], I32, name="wr_raw", align_bytes=64)
-        wr_w = keep.tile([P, PASSES, PACK, 2 * P], U8, name="wr_w", align_bytes=64)
+        wt_w = keep.tile([P, PASSES, H], I32, name="wt_w", align_bytes=64)
+        wr_w = keep.tile([P, PASSES, 2 * H], U8, name="wr_w", align_bytes=64)
         gain = keep.tile([P, PACK], F32, name="gain")
         bias = keep.tile([P, 2], F32, name="bias")
         wo_bf = keep.tile([P, 2, P, PACK], BF16, name="wo_bf", align_bytes=64)
@@ -66,11 +66,11 @@ def tile_list_triple_plausibility_readout_kernel(
                     in_=tab_scales[:, 4 * q : 4 * q + 4, :].bitcast(I32),
                 )
 
-        def load_weight_scales(engine, w, quadrants=range(4)):
-            for q in quadrants:
+        def load_weight_scales(engine, sc, src):
+            for q in range(4):
                 engine.dma_start(
-                    out=w_sc_raw[32 * q : 32 * q + 4, w, :, :].bitcast(I32),
-                    in_=(wt_scales, wr_scales)[w][:, 4 * q : 4 * q + 4, :].rearrange("a r c -> r a c").bitcast(I32),
+                    out=sc[32 * q : 32 * q + 4, :, :].bitcast(I32),
+                    in_=src[:, 4 * q : 4 * q + 4, :].rearrange("a r c -> r a c").bitcast(I32),
                 )
 
         def load_tab_pass(a):
@@ -84,28 +84,25 @@ def tile_list_triple_plausibility_readout_kernel(
             for a in range(PASSES):
                 tab[a] = words[:, a, :]
 
-        def load_wh(a):
-            wh_raw[a] = keep.tile([P, PACK, H], F32, name="wh_raw%d" % a)
-            nc.sync.dma_start(out=wh_raw[a][:], in_=wh[512 * a : 512 * (a + 1), :].rearrange("(p i) c -> p i c", i=PACK))
+        def load_wh(a, parts=1):
+            width = H // parts
+            for s in range(parts):
+                raw = ring.tile([P, PACK, width], F32, name="wh_raw", tag="wh_raw%d_%d" % (a, s), bufs=1, align_bytes=64)
+                rows = wh[512 * a : 512 * (a + 1), s * width : (s + 1) * width]
+                nc.sync.dma_start(out=raw[:], in_=rows.rearrange("(p i) c -> p i c", i=PACK))
+                wh_raw[a, s] = raw
 
         def load_wt():
-            nc.sync.dma_start(out=wt_raw[:], in_=wt_words.rearrange("a p c i -> p a (c i)").bitcast(I32))
+            nc.sync.dma_start(out=wt_w[:], in_=wt_words.rearrange("a p c i -> p a (c i)").bitcast(I32))
 
         def load_wr():
-            nc.sync.dma_start(out=wr_raw[:], in_=wr_words.rearrange("a p c -> p a c").bitcast(I32))
+            nc.sync.dma_start(out=wr_w[:].bitcast(I32), in_=wr_words.rearrange("a p c -> p a c").bitcast(I32))
 
         def load_wo():
-            rows = wo.rearrange("(q s e) n -> s q e n", s=PACK, e=RUN)
-            for s in range(PACK):
-                nc.sync.dma_start(out=wo_raw[:, s, :], in_=rows[s])
+            nc.sync.dma_start(out=wo_raw[:], in_=wo.rearrange("(p i) n -> p i n", i=PACK))
 
         def load_vectors():
-            gain_raw = keep.tile([P, PACK, RUN], F32, name="gain_raw")
-            values = g.rearrange("(q s e o) -> s q e o", s=PACK, e=RUN, o=1)
-            with nc.allow_non_contiguous_dma(reason="one gain value for each partition"):
-                for s in range(PACK):
-                    nc.sync.dma_start(out=gain_raw[:, s, 0:1], in_=values[s])
-            nc.scalar.copy(out=gain[:], in_=gain_raw[:, :, 0])
+            nc.sync.dma_start(out=gain[:], in_=g.rearrange("(p i) -> p i", i=PACK))
             nc.sync.dma_start(out=bias[:], in_=b.rearrange("(p c) -> p c", c=2))
 
         def gather_scales(name, lo=0, hi=S):
@@ -116,95 +113,93 @@ def tile_list_triple_plausibility_readout_kernel(
         def lower_rel_scales(engine):
             engine.dma_start(out=rel_sc1[0:100, :].bitcast(I32), in_=picked_sc["rel"][4:104, :].bitcast(I32))
 
-        def order_scales(engine):
-            engine.tensor_copy(
-                out=w_sc[:].bitcast(I32).rearrange("p w a s (q e) -> p (w a) s q e", e=RUN // 4),
-                in_=w_sc_raw[:].bitcast(I32).rearrange("p w a (q s e) -> p (w a) s q e", s=PACK, e=RUN // 4),
-            )
+        def cast(engine, out_ap, in_ap):
+            if engine is nc.scalar:
+                nc.scalar.copy(out=out_ap, in_=in_ap)
+            elif engine is nc.vector:
+                nc.vector.tensor_copy(out=out_ap, in_=in_ap)
+            else:
+                nc.gpsimd.tensor_scalar(out=out_ap, in0=in_ap, scalar1=1.0, scalar2=0.0, op0=ALU.mult, op1=ALU.add)
 
-        def order_wt(engine):
-            engine.tensor_copy(
-                out=wt_w[:].rearrange("p a s (q e) -> p a s q e", e=RUN),
-                in_=wt_raw[:].rearrange("p a (q s e) -> p a s q e", s=PACK, e=RUN),
-            )
+        def quantise_wh(a, engines):
+            parts = len(engines)
+            width = H // parts
+            wh_w[a] = keep.tile([P, H], U32, name="wh_w%d" % a, align_bytes=64)
+            wh_sc[a] = keep.tile([P, H], U8, name="wh_sc%d" % a, align_bytes=64)
+            for s in range(parts):
+                cols = slice(s * width, (s + 1) * width)
+                woven = ring.tile([P, width, PACK], BF16, name="wh_bf", tag="wh_bf%d_%d" % (a, s), bufs=1, align_bytes=64)
+                raw = wh_raw[a, s][:] if (a, parts - 1) in wh_raw else wh_raw[a, 0][:, :, cols]
+                cast(engines[s], woven[:].rearrange("p (c d) i -> p c i d", d=4), raw.rearrange("p i (c d) -> p c i d", d=4))
+                nc.vector.quantize_mx(out=wh_w[a][:, cols].bitcast(E4M3), scales=wh_sc[a][:, cols], in_=woven[:].rearrange("p c i -> p (c i)"))
 
-        def order_wr(engine):
-            engine.tensor_copy(
-                out=wr_w[:].bitcast(I32).rearrange("p a s (q e) -> p a s q e", e=RUN // 2),
-                in_=wr_raw[:].rearrange("p a (q s e) -> p a s q e", s=PACK, e=RUN // 2),
-            )
-
-        def quantise_wh(a):
-            woven = ring.tile([P, PACK, P, PACK], BF16, name="wh_bf", tag="wh_bf%d" % a, bufs=1, align_bytes=64)
-            wh_w[a] = keep.tile([P, PACK, P], U32, name="wh_w%d" % a, align_bytes=64)
-            wh_sc[a] = keep.tile([P, PACK, P], U8, name="wh_sc%d" % a, align_bytes=64)
-            nc.scalar.copy(
-                out=woven[:].rearrange("p s (q e) i -> p s q e i", e=RUN),
-                in_=wh_raw[a][:].rearrange("p i (q s e) -> p s q e i", s=PACK, e=RUN),
-            )
-            nc.vector.quantize_mx(
-                out=wh_w[a][:].rearrange("p s m -> p (s m)").bitcast(E4M3),
-                scales=wh_sc[a][:].rearrange("p s m -> p (s m)"),
-                in_=woven[:].rearrange("p s m i -> p (s m i)"),
-            )
-
-        def quantise_wo():
-            nc.scalar.copy(out=wo_bf[:], in_=wo_raw[:].rearrange("p i (m c) -> p c m i", c=2))
+        def quantise_wo(engine):
+            cast(engine, wo_bf[:], wo_raw[:].rearrange("p i (m c) -> p c m i", c=2))
             nc.vector.quantize_mx(out=wo_w[:].bitcast(E4M3), scales=wo_sc[:], in_=wo_bf[:].rearrange("p c m i -> p (c m i)"))
 
-        def gather_words(names, chunk, tag, bufs=1):
+        def gather_words(names, chunk, tag):
             cols = slice(chunk * CHUNK // 16, (chunk + 1) * CHUNK // 16)
-            got = ring.tile([P, len(names), PASSES, CHUNK], U32, name="picked", tag=tag, bufs=bufs, align_bytes=64)
+            got = ring.tile([P, len(names), PASSES, CHUNK], U32, name="picked", tag=tag, bufs=1, align_bytes=64)
             for x, name in enumerate(names):
                 for a in range(PASSES):
                     nc.vector.tensor_copy(out=got[:, x, a, :], in_=tab[a].bitcast(U32).indirect(lists[name][:, cols]))
                     picked[name, a, chunk] = got[:, x, a, :]
 
-        def moving(name, a, u):
+        def stationary(name, a, u):
             near = (u * P) % CHUNK
             return picked[name, a, u * P // CHUNK][:, near : near + P].bitcast(E4M3)
 
-        def project_tail(u):
+        def project_tail(u, tag=None):
             far = slice(u * P, (u + 1) * P)
-            t_ps = psum.tile([P, PACK, P], F32, name="t_ps", bufs=3)
+            t_ps = psum.tile([P, H], F32, name="t_ps", tag="ta", bufs=4)
             for a in range(PASSES):
-                for s in range(PACK):
-                    nc.tensor.matmul_mx(
-                        out=t_ps[:, s, :], lhsT=wt_w[:, a, s, :].bitcast(E4M3), lhsT_scale=w_sc[:, 0, a, s, :],
-                        rhs=moving("tail", a, u), rhs_scale=picked_sc["tail"][4 * a :, far],
-                        start=(a == 0 and s == 0), stop=(a == PASSES - 1 and s == PACK - 1),
-                    )
-            t_sb[u] = ring.tile([P, P, PACK], F32, name="t_sb", tag="t_sb%d" % u, bufs=1, align_bytes=64)
-            nc.scalar.copy(out=t_sb[u][:], in_=t_ps[:].rearrange("p s j -> p j s"))
+                nc.tensor.matmul_mx(
+                    out=t_ps[:], lhsT=stationary("tail", a, u), lhsT_scale=picked_sc["tail"][4 * a :, far],
+                    rhs=wt_w[:, a, :].bitcast(E4M3), rhs_scale=wt_sc[:, a, :],
+                    start=(a == 0), stop=(a == PASSES - 1),
+                )
+            neg_t[u] = ring.tile([P, PACK, P], F32, name="neg_t", tag=tag or "neg_t%d" % u, bufs=1, align_bytes=64)
+            nc.scalar.activation(out=neg_t[u][:], in_=t_ps[:].rearrange("j (m i) -> j i m", i=PACK), func=ACT.Copy, scale=-1.0)
 
         def project_head(u):
             far = slice(u * P, (u + 1) * P)
-            a_ps = psum.tile([P, PACK, P], F32, name="a_ps", bufs=3)
+            a_ps = psum.tile([P, H], F32, name="a_ps", tag="ta", bufs=4)
             for a in range(PASSES):
-                for s in range(PACK):
-                    nc.tensor.matmul_mx(
-                        out=a_ps[:, s, :], lhsT=wr_w[:, a, s, :].bitcast(E2M1), lhsT_scale=w_sc[:, 1, a, s, :],
-                        rhs=moving("rel", a, u), rhs_scale=(picked_sc["rel"], rel_sc1)[a][:, far],
-                        start=(a == 0 and s == 0), stop=False,
-                    )
+                nc.tensor.matmul_mx(
+                    out=a_ps[:], lhsT=stationary("rel", a, u), lhsT_scale=(picked_sc["rel"], rel_sc1)[a][:, far],
+                    rhs=wr_w[:, a, :].bitcast(E2M1), rhs_scale=wr_sc[:, a, :],
+                    start=(a == 0), stop=False,
+                )
             for a in range(PASSES):
-                for s in range(PACK):
-                    nc.tensor.matmul_mx(
-                        out=a_ps[:, s, :], lhsT=wh_w[a][:, s, :].bitcast(E4M3), lhsT_scale=wh_sc[a][:, s, :],
-                        rhs=moving("head", a, u), rhs_scale=picked_sc["head"][4 * a :, far],
-                        start=False, stop=(a == PASSES - 1 and s == PACK - 1),
-                    )
+                nc.tensor.matmul_mx(
+                    out=a_ps[:], lhsT=stationary("head", a, u), lhsT_scale=picked_sc["head"][4 * a :, far],
+                    rhs=wh_w[a][:].bitcast(E4M3), rhs_scale=wh_sc[a][:],
+                    start=False, stop=(a == PASSES - 1),
+                )
+            pos_a[u] = ring.tile([P, PACK, P], F32, name="pos_a", tag="pos_a%d" % u, bufs=1, align_bytes=64)
+            turned = a_ps[:].rearrange("j (m i) -> j i m", i=PACK)
+            if u in SUB_ON_VECTOR:
+                nc.vector.tensor_tensor(out=pos_a[u][:], in0=turned, in1=neg_t[u][:], op=ALU.add)
+            else:
+                nc.scalar.copy(out=pos_a[u][:], in_=turned)
+
+        def difference(u):
             group = [gr for gr in GROUPS if u in gr][0]
-            n = len(group) * P
             if u == group[0]:
-                diff[group] = ring.tile([P, n, PACK], F32, name="diff", bufs=5)
+                dist[group] = ring.tile([P, len(group) * P, PACK], F32, name="dist", bufs=3)
+            d_ps = psum.tile([P, PACK, P], F32, name="d_ps", bufs=2)
+            for i in range(PACK):
+                if u in SUB_ON_VECTOR:
+                    nc.tensor.matmul(out=d_ps[:, i, :], lhsT=pos_a[u][:, i, :], rhs=ident[:], is_transpose=True, start=True, stop=True)
+                else:
+                    nc.tensor.matmul(out=d_ps[:, i, :], lhsT=pos_a[u][:, i, :], rhs=ident[:], is_transpose=True, start=True, stop=False)
+                    nc.tensor.matmul(out=d_ps[:, i, :], lhsT=neg_t[u][:, i, :], rhs=ident[:], is_transpose=True, start=False, stop=True)
             at = (u - group[0]) * P
-            nc.vector.tensor_tensor(out=diff[group][:, at : at + P, :], in0=a_ps[:].rearrange("p s j -> p j s"), in1=t_sb[u][:], op=ALU.subtract)
+            nc.scalar.activation(out=dist[group][:, at : at + P, :], in_=d_ps[:].rearrange("p i j -> p j i"), func=ACT.Abs)
             if u == group[-1]:
-                dist = ring.tile([P, n, PACK], F32, name="dist", bufs=3)
-                nc.scalar.activation(out=dist[:], in_=diff[group][:], func=ACT.Abs)
+                n = len(group) * P
                 match[group] = ring.tile([P, n, PACK], F32, name="match", tag="match%d" % group[0], bufs=1, align_bytes=64)
-                nc.scalar.activation(out=match[group][:], in_=dist[:], func=ACT.Exp, scale=-1.0)
+                nc.scalar.activation(out=match[group][:], in_=dist[group][:], func=ACT.Exp, scale=-1.0)
 
         def weigh(group, tag="h_bf", bufs=2):
             n = len(group) * P
@@ -219,7 +214,7 @@ def tile_list_triple_plausibility_readout_kernel(
         def readout(group):
             n = len(group) * P
             h_w, h_sc = h_q[group]
-            y_ps = psum.tile([P, 2, n], F32, name="y_ps", bufs=2)
+            y_ps = psum.tile([P, 2, n], F32, name="y_ps", tag="y_ps", bufs=2)
             for c in range(2):
                 nc.tensor.matmul_mx(
                     out=y_ps[:, c, :], lhsT=wo_w[:, c * P : (c + 1) * P].bitcast(E4M3),
@@ -227,68 +222,74 @@ def tile_list_triple_plausibility_readout_kernel(
                     rhs=h_w[:].bitcast(E4M3), rhs_scale=h_sc[:], start=True, stop=True,
                 )
             y_sb = ring.tile([P, 2, n], F32, name="y_sb", bufs=5)
-            if group[0] in BIAS_ON_VECTOR:
-                nc.vector.tensor_tensor(out=y_sb[:], in0=y_ps[:], in1=bias[:].unsqueeze(2).to_broadcast([P, 2, n]), op=ALU.add)
-            else:
+            if group[0] in BIAS_ON_SCALAR:
                 for c in range(2):
                     nc.scalar.activation(out=y_sb[:, c, :], in_=y_ps[:, c, :], func=ACT.Identity, bias=bias[:, c : c + 1])
+            else:
+                nc.vector.tensor_tensor(out=y_sb[:], in0=y_ps[:], in1=bias[:].unsqueeze(2).to_broadcast([P, 2, n]), op=ALU.add)
             nc.sync.dma_start(out=out_v[:, :, group[0] * P : group[0] * P + n], in_=y_sb[:])
 
         nc.vector.memset(tab_sc[:].bitcast(I32), 0)
         nc.vector.memset(warm[:, 0:1], 0.0)
         nc.scalar.activation(out=warm[:, 1:2], in_=warm[:, 0:1], func=ACT.Exp)
-        nc.vector.memset(w_sc_raw[:].bitcast(I32), 0)
+        nc.vector.memset(wt_sc[:].bitcast(I32), 0)
+        nc.vector.memset(wr_sc[:].bitcast(I32), 0)
         nc.vector.memset(rel_sc1[:].bitcast(I32), 0)
         load_list("rel")
         load_tab_scales()
         load_list("tail")
         load_list("head")
         load_wh(0)
-        load_weight_scales(nc.sync, 0)
-        load_wh(1)
-        load_weight_scales(nc.sync, 1)
+        load_weight_scales(nc.sync, wt_sc, wt_scales)
+        load_tab()
+        load_weight_scales(nc.sync, wr_sc, wr_scales)
         load_wt()
+        load_wh(1)
         load_wr()
-        load_tab_pass(0)
-        load_tab_pass(1)
         gather_scales("rel")
         lower_rel_scales(nc.sync)
         load_wo()
         load_vectors()
+        make_identity(nc, ident[:])
         gather_scales("tail")
         gather_scales("head")
-        quantise_wh(0)
-        quantise_wh(1)
-        order_scales(nc.vector)
-        order_wt(nc.vector)
-        order_wr(nc.vector)
+        quantise_wh(0, [nc.scalar])
         NAMES = ["tail", "rel", "head"]
-        gather_words(NAMES, 0, "early0")
-        gather_words(NAMES, 1, "early1")
+        gather_words(NAMES, 0, "even")
+        gather_words(["tail", "rel"], 1, "odd")
         project_tail(0)
         project_tail(1)
+        quantise_wh(1, [nc.scalar])
+        gather_words(["head"], 1, "wh_bf1_0")
         project_head(0)
         project_head(1)
-        quantise_wo()
-        project_tail(2)
-        project_tail(3)
-        gather_words(NAMES, 2, "t_sb1")
-        project_head(2)
-        project_head(3)
-        project_tail(4)
-        project_tail(5)
-        weigh(GROUPS[0])
-        project_head(4)
-        project_head(5)
-        gather_words(NAMES, 3, "t_sb5")
+        project_tail(2, "wh_raw1_0")
+        project_tail(3, "neg_t3")
+        gather_words(NAMES, 2, "even")
+        quantise_wo(nc.vector)
+        for u in range(2, TILES - 2, 2):
+            difference(u - 2)
+            difference(u - 1)
+            if u > 2:
+                project_tail(u)
+            project_head(u)
+            if u > 2:
+                project_tail(u + 1)
+            project_head(u + 1)
+            weigh(GROUPS[u // 2 - 1])
+            if u == 2:
+                gather_words(NAMES, 3, "match0")
         readout(GROUPS[0])
-        weigh(GROUPS[1])
+        difference(4)
+        difference(5)
         project_tail(6)
         project_tail(7)
         project_head(6)
+        difference(6)
         project_head(7)
+        difference(7)
         readout(GROUPS[1])
-        weigh(GROUPS[2], "t_sb7", 1)
+        weigh(GROUPS[2], "neg_t7", 1)
         weigh(GROUPS[3])
         weigh(GROUPS[4])
         for group in GROUPS[2:]:

@@ -253,13 +253,13 @@ def tile_list_triple_plausibility_readout_kernel(
         make_identity(nc, ident[:])
         gather_scales("tail")
         gather_scales("head")
-        quantise_wh(0, [nc.scalar])
+        quantise_wh(0, [nc.gpsimd])
         NAMES = ["tail", "rel", "head"]
         gather_words(NAMES, 0, "even")
         gather_words(["tail", "rel"], 1, "odd")
         project_tail(0)
         project_tail(1)
-        quantise_wh(1, [nc.scalar])
+        quantise_wh(1, [nc.gpsimd])
         gather_words(["head"], 1, "wh_bf1_0")
         project_head(0)
         project_head(1)

@@ -1,7 +1,6 @@
 from contextlib import ExitStack
 
 import concourse.mybir as mybir
-from concourse.masks import make_identity
 
 K, H, N, T, S = 1024, 512, 256, 2048, 1024
 FLOPS = 2 * (3 * K * H * S + H * N * S)
@@ -21,11 +20,15 @@ P = 128
 PACK = 4
 PASSES = K // (P * PACK)
 CHUNK = 256
+CHUNKS = S // CHUNK
 TILES = S // P
+RUN = 8
+BLOCKS = H // (PACK * RUN)
 GROUPS = [(0, 1), (2, 3), (4, 5), (6,), (7,)]
-SUB_ON_VECTOR = (6,7)
-GAIN_ON_GPSIMD = ()
-BIAS_ON_SCALAR = (2,4,6,7)
+SUB_ON_GPSIMD = (0, 1, 2, 3)
+GAIN_ON_GPSIMD = (0, 1, 2)
+TAIL_ON_VECTOR = ()
+BIAS_ON_SCALAR = (2, 4, 6, 7)
 
 
 def tile_list_triple_plausibility_readout_kernel(
@@ -34,26 +37,27 @@ def tile_list_triple_plausibility_readout_kernel(
     nc = tc.nc
     with ExitStack() as ctx:
         keep = ctx.enter_context(tc.tile_pool(name="keep", bufs=1))
-        ring = ctx.enter_context(tc.tile_pool(name="ring", bufs=2))
-        psum = ctx.enter_context(tc.psum_pool(name="psum", bufs=2))
+        psum = ctx.enter_context(tc.psum_pool(name="psum", bufs=1))
 
-        lists, picked_sc, picked, wh_raw, wh_bf, wh_w, wh_sc, tab = {}, {}, {}, {}, {}, {}, {}, {}
-        neg_t, pos_a, dist, match, h_q = {}, {}, {}, {}, {}
+        lists, picked, wh_raw, wh_bf, tab = {}, {}, {}, {}, {}
+        t_sb, a_ps, diff, match, h_bf, h_q, wo_q = {}, {}, {}, {}, {}, {}, {}
         tab_sc = keep.tile([P, T], U8, name="tab_sc", align_bytes=64)
         wt_sc = keep.tile([P, PASSES, H], U8, name="wt_sc", align_bytes=64)
         wr_sc = keep.tile([P, PASSES, H], U8, name="wr_sc", align_bytes=64)
         rel_sc1 = keep.tile([P, S], U8, name="rel_sc1", align_bytes=64)
-        warm = keep.tile([P, 2], F32, name="warm")
-        ident = keep.tile([P, P], F32, name="ident")
-        wo_raw = keep.tile([P, PACK, N], F32, name="wo_raw")
-        wt_w = keep.tile([P, PASSES, H], I32, name="wt_w", align_bytes=64)
+        wt_w = keep.tile([P, PASSES, 4 * H], U8, name="wt_w", align_bytes=64)
         wr_w = keep.tile([P, PASSES, 2 * H], U8, name="wr_w", align_bytes=64)
-        gain = keep.tile([P, PACK], F32, name="gain")
+        wh_w = keep.tile([P, PASSES, H], U32, name="wh_w", align_bytes=64)
+        wh_sc = keep.tile([P, PASSES, H], U8, name="wh_sc", align_bytes=64)
+        wo_raw = keep.tile([P, PACK, N], F32, name="wo_raw")
+        gain = keep.tile([P, PACK, 8], F32, name="gain")
+        gains = keep.tile([P, PACK], F32, name="gains")
+        zero = keep.tile([P, PACK], F32, name="zero")
         bias = keep.tile([P, 2], F32, name="bias")
-        wo_bf = keep.tile([P, 2, P, PACK], BF16, name="wo_bf", align_bytes=64)
-        wo_w = keep.tile([P, N], U32, name="wo_w", align_bytes=64)
-        wo_sc = keep.tile([P, N], U8, name="wo_sc", align_bytes=64)
         out_v = out.rearrange("(p c) j -> p c j", c=2)
+
+        def own(shape, dtype, tag):
+            return keep.tile(shape, dtype, name=tag, tag=tag, align_bytes=64)
 
         def load_list(name):
             lists[name] = keep.tile([P, S // 16], U16, name="list_" + name)
@@ -66,162 +70,175 @@ def tile_list_triple_plausibility_readout_kernel(
                     in_=tab_scales[:, 4 * q : 4 * q + 4, :].bitcast(I32),
                 )
 
-        def load_weight_scales(engine, sc, src):
+        def load_weight_scales(sc, src):
             for q in range(4):
-                engine.dma_start(
+                nc.sync.dma_start(
                     out=sc[32 * q : 32 * q + 4, :, :].bitcast(I32),
                     in_=src[:, 4 * q : 4 * q + 4, :].rearrange("a r c -> r a c").bitcast(I32),
                 )
 
-        def load_tab_pass(a):
-            words = keep.tile([P, T], I32, name="tab%d" % a, align_bytes=64)
-            nc.sync.dma_start(out=words[:], in_=tab_words[a].rearrange("p t i -> p (t i)").bitcast(I32))
-            tab[a] = words[:]
+        def load_tab(a):
+            tab[a] = keep.tile([P, T], I32, name="tab%d" % a, align_bytes=64)
+            nc.sync.dma_start(out=tab[a][:], in_=tab_words[a].rearrange("p t i -> p (t i)").bitcast(I32))
 
-        def load_tab():
-            words = keep.tile([P, PASSES, T], I32, name="tab", align_bytes=64)
-            nc.sync.dma_start(out=words[:], in_=tab_words.rearrange("a p t i -> p a (t i)").bitcast(I32))
-            for a in range(PASSES):
-                tab[a] = words[:, a, :]
-
-        def load_wh(a, parts=1):
-            width = H // parts
-            for s in range(parts):
-                raw = ring.tile([P, PACK, width], F32, name="wh_raw", tag="wh_raw%d_%d" % (a, s), bufs=1, align_bytes=64)
-                rows = wh[512 * a : 512 * (a + 1), s * width : (s + 1) * width]
-                nc.sync.dma_start(out=raw[:], in_=rows.rearrange("(p i) c -> p i c", i=PACK))
-                wh_raw[a, s] = raw
+        def load_wh(a):
+            wh_raw[a] = own([P, PACK, H], F32, "wh_raw%d" % a)
+            nc.sync.dma_start(out=wh_raw[a][:], in_=wh[512 * a : 512 * (a + 1), :].rearrange("(p i) c -> p i c", i=PACK))
 
         def load_wt():
-            nc.sync.dma_start(out=wt_w[:], in_=wt_words.rearrange("a p c i -> p a (c i)").bitcast(I32))
+            nc.sync.dma_start(out=wt_w[:].bitcast(I32), in_=wt_words.rearrange("a p c i -> p a (c i)").bitcast(I32))
 
         def load_wr():
             nc.sync.dma_start(out=wr_w[:].bitcast(I32), in_=wr_words.rearrange("a p c -> p a c").bitcast(I32))
 
         def load_wo():
-            nc.sync.dma_start(out=wo_raw[:], in_=wo.rearrange("(p i) n -> p i n", i=PACK))
+            rows = wo.rearrange("(q i e) n -> i q e n", i=PACK, e=RUN)
+            for i in range(PACK):
+                nc.sync.dma_start(out=wo_raw[:, i, :], in_=rows[i])
 
-        def load_vectors():
-            nc.sync.dma_start(out=gain[:], in_=g.rearrange("(p i) -> p i", i=PACK))
+        def load_gain():
+            rows = g.rearrange("(q i e o) -> i q e o", i=PACK, e=RUN, o=1)
+            with nc.allow_non_contiguous_dma(reason="one gain for each partition"):
+                for i in range(PACK):
+                    nc.scalar.dma_start(out=gain[:, i, 0:1], in_=rows[i])
+
+        def load_bias():
             nc.sync.dma_start(out=bias[:], in_=b.rearrange("(p c) -> p c", c=2))
 
-        def gather_scales(name, lo=0, hi=S):
-            if lo == 0:
-                picked_sc[name] = keep.tile([P, S], U8, name="sc_" + name, align_bytes=64)
-            nc.vector.tensor_copy(out=picked_sc[name][:, lo:hi], in_=tab_sc[:].indirect(lists[name][:, lo // 16 : hi // 16]))
+        def deal(src, width, name, engine):
+            dealt = keep.tile([P, PASSES, width], U8, name=name, align_bytes=64)
+            engine.tensor_copy(
+                out=dealt[:].bitcast(I32).rearrange("p a (i q e) -> p a i q e", i=PACK, q=BLOCKS),
+                in_=src[:].bitcast(I32).rearrange("p a (q i e) -> p a i q e", i=PACK, q=BLOCKS),
+            )
+            return dealt
 
-        def lower_rel_scales(engine):
-            engine.dma_start(out=rel_sc1[0:100, :].bitcast(I32), in_=picked_sc["rel"][4:104, :].bitcast(I32))
+        def round_wh(a, on_scalar):
+            wh_bf[a] = own([P, PACK, BLOCKS, RUN, PACK], BF16, "wh_bf%d" % a)
+            raw = wh_raw[a][:].rearrange("p k (q i e) -> p i q e k", i=PACK, e=RUN)
+            if on_scalar:
+                nc.scalar.copy(out=wh_bf[a][:, :on_scalar, :, :, :], in_=raw[:, :on_scalar, :, :, :])
+            for i in range(on_scalar, PACK):
+                nc.gpsimd.tensor_scalar(out=wh_bf[a][:, i, :, :, :], in0=raw[:, i, :, :, :], scalar1=1.0, scalar2=0.0, op0=ALU.mult, op1=ALU.add)
 
-        def cast(engine, out_ap, in_ap):
-            if engine is nc.scalar:
-                nc.scalar.copy(out=out_ap, in_=in_ap)
-            elif engine is nc.vector:
-                nc.vector.tensor_copy(out=out_ap, in_=in_ap)
+        def quantise_wh(a):
+            nc.vector.quantize_mx(out=wh_w[:, a, :].bitcast(E4M3), scales=wh_sc[:, a, :], in_=wh_bf[a][:].rearrange("p i q e k -> p (i q e k)"))
+
+        def round_wo(engine, tag):
+            wo_q["bf"] = own([P, 2, P, PACK], BF16, tag)
+            raw = wo_raw[:].rearrange("p i (m c) -> p c m i", c=2)
+            if engine is nc.gpsimd:
+                for c in range(2):
+                    nc.gpsimd.tensor_scalar(out=wo_q["bf"][:, c, :, :], in0=raw[:, c, :, :], scalar1=1.0, scalar2=0.0, op0=ALU.mult, op1=ALU.add)
+            elif engine is nc.scalar:
+                nc.scalar.copy(out=wo_q["bf"][:], in_=raw)
             else:
-                nc.gpsimd.tensor_scalar(out=out_ap, in0=in_ap, scalar1=1.0, scalar2=0.0, op0=ALU.mult, op1=ALU.add)
+                nc.vector.tensor_copy(out=wo_q["bf"][:], in_=raw)
 
-        def quantise_wh(a, engines):
-            parts = len(engines)
-            width = H // parts
-            wh_w[a] = keep.tile([P, H], U32, name="wh_w%d" % a, align_bytes=64)
-            wh_sc[a] = keep.tile([P, H], U8, name="wh_sc%d" % a, align_bytes=64)
-            for s in range(parts):
-                cols = slice(s * width, (s + 1) * width)
-                woven = ring.tile([P, width, PACK], BF16, name="wh_bf", tag="wh_bf%d_%d" % (a, s), bufs=1, align_bytes=64)
-                raw = wh_raw[a, s][:] if (a, parts - 1) in wh_raw else wh_raw[a, 0][:, :, cols]
-                cast(engines[s], woven[:].rearrange("p (c d) i -> p c i d", d=4), raw.rearrange("p i (c d) -> p c i d", d=4))
-                nc.vector.quantize_mx(out=wh_w[a][:, cols].bitcast(E4M3), scales=wh_sc[a][:, cols], in_=woven[:].rearrange("p c i -> p (c i)"))
+        def quantise_wo(tag):
+            wo_q["w"] = own([P, N], U32, tag)
+            wo_q["sc"] = own([P, N], U8, "wo_sc")
+            nc.vector.quantize_mx(out=wo_q["w"][:].bitcast(E4M3), scales=wo_q["sc"][:], in_=wo_q["bf"][:].rearrange("p c m i -> p (c m i)"))
 
-        def quantise_wo(engine):
-            cast(engine, wo_bf[:], wo_raw[:].rearrange("p i (m c) -> p c m i", c=2))
-            nc.vector.quantize_mx(out=wo_w[:].bitcast(E4M3), scales=wo_sc[:], in_=wo_bf[:].rearrange("p c m i -> p (c m i)"))
+        def gather(jobs, tag):
+            got = own([P, CHUNK * sum(job[3] for job in jobs)], U32, tag)
+            at = 0
+            for name, a, c0, n in jobs:
+                offsets = lists[name][:, c0 * CHUNK // 16 : (c0 + n) * CHUNK // 16]
+                nc.vector.tensor_copy(out=got[:, at : at + n * CHUNK], in_=tab[a][:].bitcast(U32).indirect(offsets))
+                for c in range(n):
+                    picked[name, a, c0 + c] = got[:, at + c * CHUNK : at + (c + 1) * CHUNK]
+                at = at + n * CHUNK
 
-        def gather_words(names, chunk, tag):
-            cols = slice(chunk * CHUNK // 16, (chunk + 1) * CHUNK // 16)
-            got = ring.tile([P, len(names), PASSES, CHUNK], U32, name="picked", tag=tag, bufs=1, align_bytes=64)
-            for x, name in enumerate(names):
-                for a in range(PASSES):
-                    nc.vector.tensor_copy(out=got[:, x, a, :], in_=tab[a].bitcast(U32).indirect(lists[name][:, cols]))
-                    picked[name, a, chunk] = got[:, x, a, :]
+        def gather_scales(name):
+            picked[name] = own([P, S], U8, "sc_" + name)
+            nc.vector.tensor_copy(out=picked[name][:], in_=tab_sc[:].indirect(lists[name][:]))
 
-        def stationary(name, a, u):
+        def lower_rel_scales():
+            nc.sync.dma_start(out=rel_sc1[0:100, :].bitcast(I32), in_=picked["rel"][4:104, :].bitcast(I32))
+
+        def words(name, a, u):
             near = (u * P) % CHUNK
             return picked[name, a, u * P // CHUNK][:, near : near + P].bitcast(E4M3)
 
-        def project_tail(u, tag=None):
+        def project_tail(u, bank, tag=None):
             far = slice(u * P, (u + 1) * P)
-            t_ps = psum.tile([P, H], F32, name="t_ps", tag="ta", bufs=4)
+            t_ps = psum.tile([P, PACK, P], F32, name="t_ps", tag="bank%d" % bank)
             for a in range(PASSES):
-                nc.tensor.matmul_mx(
-                    out=t_ps[:], lhsT=stationary("tail", a, u), lhsT_scale=picked_sc["tail"][4 * a :, far],
-                    rhs=wt_w[:, a, :].bitcast(E4M3), rhs_scale=wt_sc[:, a, :],
-                    start=(a == 0), stop=(a == PASSES - 1),
-                )
-            neg_t[u] = ring.tile([P, PACK, P], F32, name="neg_t", tag=tag or "neg_t%d" % u, bufs=1, align_bytes=64)
-            nc.scalar.activation(out=neg_t[u][:], in_=t_ps[:].rearrange("j (m i) -> j i m", i=PACK), func=ACT.Copy, scale=-1.0)
-
-        def project_head(u):
-            far = slice(u * P, (u + 1) * P)
-            a_ps = psum.tile([P, H], F32, name="a_ps", tag="ta", bufs=4)
-            for a in range(PASSES):
-                nc.tensor.matmul_mx(
-                    out=a_ps[:], lhsT=stationary("rel", a, u), lhsT_scale=(picked_sc["rel"], rel_sc1)[a][:, far],
-                    rhs=wr_w[:, a, :].bitcast(E2M1), rhs_scale=wr_sc[:, a, :],
-                    start=(a == 0), stop=False,
-                )
-            for a in range(PASSES):
-                nc.tensor.matmul_mx(
-                    out=a_ps[:], lhsT=stationary("head", a, u), lhsT_scale=picked_sc["head"][4 * a :, far],
-                    rhs=wh_w[a][:].bitcast(E4M3), rhs_scale=wh_sc[a][:],
-                    start=False, stop=(a == PASSES - 1),
-                )
-            pos_a[u] = ring.tile([P, PACK, P], F32, name="pos_a", tag="pos_a%d" % u, bufs=1, align_bytes=64)
-            turned = a_ps[:].rearrange("j (m i) -> j i m", i=PACK)
-            if u in SUB_ON_VECTOR:
-                nc.vector.tensor_tensor(out=pos_a[u][:], in0=turned, in1=neg_t[u][:], op=ALU.add)
+                for i in range(PACK):
+                    cols = slice(i * P, (i + 1) * P)
+                    nc.tensor.matmul_mx(
+                        out=t_ps[:, i, :], lhsT=wt_dw[:, a, 4 * i * P : 4 * (i + 1) * P].bitcast(E4M3), lhsT_scale=wt_ds[:, a, cols],
+                        rhs=words("tail", a, u), rhs_scale=picked["tail"][4 * a :, far],
+                        start=(a == 0 and i == 0), stop=(a == PASSES - 1 and i == PACK - 1),
+                    )
+            t_sb[u] = own([P, P, PACK], F32, tag or "t_sb%d" % u)
+            if u in TAIL_ON_VECTOR:
+                nc.vector.tensor_copy(out=t_sb[u][:], in_=t_ps[:].rearrange("p i j -> p j i"))
             else:
-                nc.scalar.copy(out=pos_a[u][:], in_=turned)
+                nc.scalar.copy(out=t_sb[u][:], in_=t_ps[:].rearrange("p i j -> p j i"))
 
-        def difference(u):
+        def project_a(u, bank):
+            far = slice(u * P, (u + 1) * P)
+            a_ps[u] = psum.tile([P, PACK, P], F32, name="a_ps", tag="bank%d" % bank)
+            for a in range(PASSES):
+                for i in range(PACK):
+                    nc.tensor.matmul_mx(
+                        out=a_ps[u][:, i, :], lhsT=wr_dw[:, a, 2 * i * P : 2 * (i + 1) * P].bitcast(E2M1), lhsT_scale=wr_ds[:, a, i * P : (i + 1) * P],
+                        rhs=words("rel", a, u), rhs_scale=(picked["rel"], rel_sc1)[a][:, far],
+                        start=(a == 0 and i == 0), stop=False,
+                    )
+            for a in range(PASSES):
+                for i in range(PACK):
+                    cols = slice(i * P, (i + 1) * P)
+                    nc.tensor.matmul_mx(
+                        out=a_ps[u][:, i, :], lhsT=wh_w[:, a, cols].bitcast(E4M3), lhsT_scale=wh_sc[:, a, cols],
+                        rhs=words("head", a, u), rhs_scale=picked["head"][4 * a :, far],
+                        start=False, stop=(a == PASSES - 1 and i == PACK - 1),
+                    )
+
+        def subtract(u):
+            diff[u] = own([P, P, PACK], F32, "diff%d" % u)
+            woven = a_ps[u][:].rearrange("p i j -> p j i")
+            if u in SUB_ON_GPSIMD:
+                a_sb = own([P, P, PACK], F32, "a_sb%d" % u)
+                nc.scalar.copy(out=a_sb[:], in_=woven)
+                nc.gpsimd.tensor_tensor(out=diff[u][:], in0=a_sb[:], in1=t_sb[u][:], op=ALU.subtract)
+            else:
+                nc.vector.tensor_tensor(out=diff[u][:], in0=woven, in1=t_sb[u][:], op=ALU.subtract)
+
+        def exponential(u):
+            dist = own([P, P, PACK], F32, "dist%d" % u)
+            nc.scalar.activation(out=dist[:], in_=diff[u][:], func=ACT.Abs)
+            match[u] = own([P, P, PACK], F32, "match%d" % u)
+            nc.scalar.activation(out=match[u][:], in_=dist[:], func=ACT.Exp, scale=-1.0)
+
+        def weigh(u):
             group = [gr for gr in GROUPS if u in gr][0]
             if u == group[0]:
-                dist[group] = ring.tile([P, len(group) * P, PACK], F32, name="dist", bufs=3)
-            d_ps = psum.tile([P, PACK, P], F32, name="d_ps", bufs=2)
-            for i in range(PACK):
-                if u in SUB_ON_VECTOR:
-                    nc.tensor.matmul(out=d_ps[:, i, :], lhsT=pos_a[u][:, i, :], rhs=ident[:], is_transpose=True, start=True, stop=True)
-                else:
-                    nc.tensor.matmul(out=d_ps[:, i, :], lhsT=pos_a[u][:, i, :], rhs=ident[:], is_transpose=True, start=True, stop=False)
-                    nc.tensor.matmul(out=d_ps[:, i, :], lhsT=neg_t[u][:, i, :], rhs=ident[:], is_transpose=True, start=False, stop=True)
+                h_bf[group] = own([P, len(group) * P, PACK], BF16, "h_bf%d" % u)
             at = (u - group[0]) * P
-            nc.scalar.activation(out=dist[group][:, at : at + P, :], in_=d_ps[:].rearrange("p i j -> p j i"), func=ACT.Abs)
-            if u == group[-1]:
-                n = len(group) * P
-                match[group] = ring.tile([P, n, PACK], F32, name="match", tag="match%d" % group[0], bufs=1, align_bytes=64)
-                nc.scalar.activation(out=match[group][:], in_=dist[group][:], func=ACT.Exp, scale=-1.0)
+            engine = nc.gpsimd if u in GAIN_ON_GPSIMD else nc.vector
+            engine.tensor_tensor(out=h_bf[group][:, at : at + P, :], in0=match[u][:], in1=gains[:].unsqueeze(1).to_broadcast([P, P, PACK]), op=ALU.mult)
 
-        def weigh(group, tag="h_bf", bufs=2):
+        def quantise_h(group, tag=None):
             n = len(group) * P
-            h_bf = ring.tile([P, n, PACK], BF16, name="h_bf", tag=tag, bufs=bufs, align_bytes=64)
-            engine = nc.gpsimd if group[0] in GAIN_ON_GPSIMD else nc.vector
-            engine.tensor_tensor(out=h_bf[:], in0=match[group][:], in1=gain[:].unsqueeze(1).to_broadcast([P, n, PACK]), op=ALU.mult)
-            h_w = ring.tile([P, n], U32, name="h_w", align_bytes=64)
-            h_sc = ring.tile([P, n], U8, name="h_sc", align_bytes=64)
-            nc.vector.quantize_mx(out=h_w[:].bitcast(E4M3), scales=h_sc[:], in_=h_bf[:].rearrange("p j i -> p (j i)"))
+            h_w = own([P, n], U32, tag or "h_w%d" % group[0])
+            h_sc = own([P, n], U8, "h_sc%d" % group[0])
+            nc.vector.quantize_mx(out=h_w[:].bitcast(E4M3), scales=h_sc[:], in_=h_bf[group][:].rearrange("p j i -> p (j i)"))
             h_q[group] = (h_w, h_sc)
 
-        def readout(group):
+        def readout(group, bank):
             n = len(group) * P
             h_w, h_sc = h_q[group]
-            y_ps = psum.tile([P, 2, n], F32, name="y_ps", tag="y_ps", bufs=2)
+            y_ps = psum.tile([P, 2, n], F32, name="y_ps", tag="bank%d" % bank)
             for c in range(2):
                 nc.tensor.matmul_mx(
-                    out=y_ps[:, c, :], lhsT=wo_w[:, c * P : (c + 1) * P].bitcast(E4M3),
-                    lhsT_scale=wo_sc[:, c * P : (c + 1) * P],
+                    out=y_ps[:, c, :], lhsT=wo_q["w"][:, c * P : (c + 1) * P].bitcast(E4M3),
+                    lhsT_scale=wo_q["sc"][:, c * P : (c + 1) * P],
                     rhs=h_w[:].bitcast(E4M3), rhs_scale=h_sc[:], start=True, stop=True,
                 )
-            y_sb = ring.tile([P, 2, n], F32, name="y_sb", bufs=5)
+            y_sb = own([P, 2, n], F32, "y_sb%d" % group[0])
             if group[0] in BIAS_ON_SCALAR:
                 for c in range(2):
                     nc.scalar.activation(out=y_sb[:, c, :], in_=y_ps[:, c, :], func=ACT.Identity, bias=bias[:, c : c + 1])
@@ -229,68 +246,84 @@ def tile_list_triple_plausibility_readout_kernel(
                 nc.vector.tensor_tensor(out=y_sb[:], in0=y_ps[:], in1=bias[:].unsqueeze(2).to_broadcast([P, 2, n]), op=ALU.add)
             nc.sync.dma_start(out=out_v[:, :, group[0] * P : group[0] * P + n], in_=y_sb[:])
 
-        nc.vector.memset(tab_sc[:].bitcast(I32), 0)
-        nc.vector.memset(warm[:, 0:1], 0.0)
-        nc.scalar.activation(out=warm[:, 1:2], in_=warm[:, 0:1], func=ACT.Exp)
-        nc.vector.memset(wt_sc[:].bitcast(I32), 0)
-        nc.vector.memset(wr_sc[:].bitcast(I32), 0)
-        nc.vector.memset(rel_sc1[:].bitcast(I32), 0)
-        load_list("rel")
-        load_tab_scales()
+        for plane in (tab_sc, wt_sc, wr_sc, rel_sc1):
+            nc.vector.memset(plane[:].bitcast(I32), 0)
+        load_gain()
+        nc.vector.memset(zero[:], 0.0)
+        nc.gpsimd.tensor_tensor(out=gains[:], in0=gain[:, :, 0], in1=zero[:], op=ALU.add)
         load_list("tail")
+        load_tab(0)
+        load_tab_scales()
+        load_tab(1)
+        load_list("rel")
+        load_weight_scales(wt_sc, wt_scales)
+        load_wt()
         load_list("head")
         load_wh(0)
-        load_weight_scales(nc.sync, wt_sc, wt_scales)
-        load_tab()
-        load_weight_scales(nc.sync, wr_sc, wr_scales)
-        load_wt()
         load_wh(1)
-        load_wr()
-        gather_scales("rel")
-        lower_rel_scales(nc.sync)
-        load_wo()
-        load_vectors()
-        make_identity(nc, ident[:])
+        gather([("tail", 0, 0, 2)], "tail0")
         gather_scales("tail")
+        gather([("tail", 1, 0, 1), ("tail", 1, 1, 1)], "tail1")
+        gather_scales("rel")
+        load_weight_scales(wr_sc, wr_scales)
+        load_wr()
+        lower_rel_scales()
+        load_wo()
+        load_bias()
         gather_scales("head")
-        quantise_wh(0, [nc.gpsimd])
-        NAMES = ["tail", "rel", "head"]
-        gather_words(NAMES, 0, "even")
-        gather_words(["tail", "rel"], 1, "odd")
-        project_tail(0)
-        project_tail(1)
-        quantise_wh(1, [nc.gpsimd])
-        gather_words(["head"], 1, "wh_bf1_0")
-        project_head(0)
-        project_head(1)
-        project_tail(2, "wh_raw1_0")
-        project_tail(3, "neg_t3")
-        gather_words(NAMES, 2, "even")
-        quantise_wo(nc.vector)
-        for u in range(2, TILES - 2, 2):
-            difference(u - 2)
-            difference(u - 1)
-            if u > 2:
-                project_tail(u)
-            project_head(u)
-            if u > 2:
-                project_tail(u + 1)
-            project_head(u + 1)
-            weigh(GROUPS[u // 2 - 1])
-            if u == 2:
-                gather_words(NAMES, 3, "match0")
-        readout(GROUPS[0])
-        difference(4)
-        difference(5)
-        project_tail(6)
-        project_tail(7)
-        project_head(6)
-        difference(6)
-        project_head(7)
-        difference(7)
-        readout(GROUPS[1])
-        weigh(GROUPS[2], "neg_t7", 1)
-        weigh(GROUPS[3])
-        weigh(GROUPS[4])
-        for group in GROUPS[2:]:
-            readout(group)
+        gather([(n, a, 0, 1) for n in ("rel", "head") for a in (0, 1)], "first")
+        wt_ds = deal(wt_sc, H, "wt_ds", nc.gpsimd)
+        wt_dw = deal(wt_w, 4 * H, "wt_dw", nc.gpsimd)
+        project_tail(0, 0)
+        project_tail(1, 1)
+        round_wh(0, 0)
+        round_wh(1, 4)
+        project_tail(2, 2, "wh_raw1")
+        project_tail(3, 3, "wh_raw0")
+        wr_ds = deal(wr_sc, H, "wr_ds", nc.gpsimd)
+        wr_dw = deal(wr_w, 2 * H, "wr_dw", nc.gpsimd)
+        quantise_wh(0)
+        quantise_wh(1)
+        LATE = [(n, a, c, 1) for n, c in (("rel", 1), ("head", 1), ("tail", 2), ("rel", 2), ("head", 2), ("tail", 3), ("rel", 3), ("head", 3)) for a in (0, 1)]
+        gather(LATE[:16], "wh_bf1")
+        G = GROUPS
+        for u in range(4):
+            project_a(u, 4 + u)
+            subtract(u)
+            if u > 0:
+                exponential(u - 1)
+        round_wo(nc.gpsimd, "a_sb1")
+        project_tail(4, 4)
+        project_tail(5, 5)
+        exponential(3)
+        for u in range(4):
+            weigh(u)
+        project_a(4, 0)
+        subtract(4)
+        project_a(5, 1)
+        subtract(5)
+
+        project_tail(6, 6)
+        project_tail(7, 7)
+        exponential(4)
+        project_a(6, 2)
+        subtract(6)
+        exponential(5)
+        project_a(7, 3)
+        subtract(7)
+        exponential(6)
+        exponential(7)
+        quantise_wo("t_sb6")
+        quantise_h(G[0], "t_sb7")
+        quantise_h(G[1])
+        weigh(4)
+        weigh(5)
+        readout(G[0], 4)
+        quantise_h(G[2])
+        weigh(6)
+        readout(G[1], 5)
+        quantise_h(G[3])
+        weigh(7)
+        quantise_h(G[4])
+        for x in (2, 3, 4):
+            readout(G[x], x + 4 - 8 * (x // 4))

@@ -26,9 +26,8 @@ RUN = 8
 BLOCKS = H // (PACK * RUN)
 GROUPS = [(0, 1), (2, 3), (4, 5), (6,), (7,)]
 SUB_ON_GPSIMD = (0, 1, 2, 3)
-GAIN_ON_GPSIMD = (0, 1, 2)
-TAIL_ON_VECTOR = ()
-BIAS_ON_SCALAR = (2, 4, 6, 7)
+GAIN_ON_GPSIMD = (0, 1, 2, 3)
+BIAS_ON_SCALAR = (0, 2, 4, 6, 7)
 
 
 def tile_list_triple_plausibility_readout_kernel(
@@ -54,7 +53,7 @@ def tile_list_triple_plausibility_readout_kernel(
         gains = keep.tile([P, PACK], F32, name="gains")
         zero = keep.tile([P, PACK], F32, name="zero")
         bias = keep.tile([P, 2], F32, name="bias")
-        out_v = out.rearrange("(p c) j -> p c j", c=2)
+        out_v = out.rearrange("(c p) j -> p c j", c=2)
 
         def own(shape, dtype, tag):
             return keep.tile(shape, dtype, name=tag, tag=tag, align_bytes=64)
@@ -103,7 +102,8 @@ def tile_list_triple_plausibility_readout_kernel(
                     nc.scalar.dma_start(out=gain[:, i, 0:1], in_=rows[i])
 
         def load_bias():
-            nc.sync.dma_start(out=bias[:], in_=b.rearrange("(p c) -> p c", c=2))
+            with nc.allow_non_contiguous_dma(reason="two biases for each partition"):
+                nc.sync.dma_start(out=bias[:], in_=b.rearrange("(c p) -> p c", c=2))
 
         def deal(src, width, name, engine):
             dealt = keep.tile([P, PASSES, width], U8, name=name, align_bytes=64)
@@ -125,20 +125,20 @@ def tile_list_triple_plausibility_readout_kernel(
             nc.vector.quantize_mx(out=wh_w[:, a, :].bitcast(E4M3), scales=wh_sc[:, a, :], in_=wh_bf[a][:].rearrange("p i q e k -> p (i q e k)"))
 
         def round_wo(engine, tag):
-            wo_q["bf"] = own([P, 2, P, PACK], BF16, tag)
-            raw = wo_raw[:].rearrange("p i (m c) -> p c m i", c=2)
+            wo_q["bf"] = own([P, N, PACK], BF16, tag)
+            woven = wo_q["bf"][:].rearrange("p (c d) i -> p c i d", d=4)
+            raw = wo_raw[:].rearrange("p i (c d) -> p c i d", d=4)
             if engine is nc.gpsimd:
-                for c in range(2):
-                    nc.gpsimd.tensor_scalar(out=wo_q["bf"][:, c, :, :], in0=raw[:, c, :, :], scalar1=1.0, scalar2=0.0, op0=ALU.mult, op1=ALU.add)
+                nc.gpsimd.tensor_scalar(out=woven, in0=raw, scalar1=1.0, scalar2=0.0, op0=ALU.mult, op1=ALU.add)
             elif engine is nc.scalar:
-                nc.scalar.copy(out=wo_q["bf"][:], in_=raw)
+                nc.scalar.copy(out=woven, in_=raw)
             else:
-                nc.vector.tensor_copy(out=wo_q["bf"][:], in_=raw)
+                nc.vector.tensor_copy(out=woven, in_=raw)
 
         def quantise_wo(tag):
             wo_q["w"] = own([P, N], U32, tag)
             wo_q["sc"] = own([P, N], U8, "wo_sc")
-            nc.vector.quantize_mx(out=wo_q["w"][:].bitcast(E4M3), scales=wo_q["sc"][:], in_=wo_q["bf"][:].rearrange("p c m i -> p (c m i)"))
+            nc.vector.quantize_mx(out=wo_q["w"][:].bitcast(E4M3), scales=wo_q["sc"][:], in_=wo_q["bf"][:].rearrange("p n i -> p (n i)"))
 
         def gather(jobs, tag):
             got = own([P, CHUNK * sum(job[3] for job in jobs)], U32, tag)
@@ -157,69 +157,81 @@ def tile_list_triple_plausibility_readout_kernel(
         def lower_rel_scales():
             nc.sync.dma_start(out=rel_sc1[0:100, :].bitcast(I32), in_=picked["rel"][4:104, :].bitcast(I32))
 
-        def words(name, a, u):
-            near = (u * P) % CHUNK
-            return picked[name, a, u * P // CHUNK][:, near : near + P].bitcast(E4M3)
+        def banks_of(group):
+            slots = PACK // len(group)
+            return [(first, slots) for first in range(0, PACK, slots)]
 
-        def project_tail(u, bank, tag=None):
-            far = slice(u * P, (u + 1) * P)
-            t_ps = psum.tile([P, PACK, P], F32, name="t_ps", tag="bank%d" % bank)
+        def words(name, a, lo, n):
+            return picked[name, a, lo // CHUNK][:, lo % CHUNK : lo % CHUNK + n].bitcast(E4M3)
+
+        def project_tail(group, banks, shared=None):
+            lo, n = group[0] * P, len(group) * P
+            for x, (first, slots) in enumerate(banks_of(group)):
+                t_ps = psum.tile([P, slots, n], F32, name="t_ps", tag="bank%d" % banks[x])
+                for a in range(PASSES):
+                    for i in range(first, first + slots):
+                        nc.tensor.matmul_mx(
+                            out=t_ps[:, i - first, :], lhsT=wt_dw[:, a, 4 * i * P : 4 * (i + 1) * P].bitcast(E4M3), lhsT_scale=wt_ds[:, a, i * P : (i + 1) * P],
+                            rhs=words("tail", a, lo, n), rhs_scale=picked["tail"][4 * a :, lo : lo + n],
+                            start=(a == 0 and i == first), stop=(a == PASSES - 1 and i == first + slots - 1),
+                        )
+                t_sb[group, x] = shared[:, group[0] + x, :, :] if shared is not None else own([P, n, slots], F32, "t_sb%d" % (group[0] + x))[:]
+                nc.scalar.copy(out=t_sb[group, x], in_=t_ps[:].rearrange("p i j -> p j i"))
+
+        def project_a(group, x, bank):
+            lo, n = group[0] * P, len(group) * P
+            first, slots = banks_of(group)[x]
+            a_ps[group, x] = psum.tile([P, slots, n], F32, name="a_ps", tag="bank%d" % bank)
             for a in range(PASSES):
-                for i in range(PACK):
+                for i in range(first, first + slots):
+                    for at in range(0, n, P):
+                        nc.tensor.matmul_mx(
+                            out=a_ps[group, x][:, i - first, at : at + P], lhsT=wr_dw[:, a, 2 * i * P : 2 * (i + 1) * P].bitcast(E2M1), lhsT_scale=wr_ds[:, a, i * P : (i + 1) * P],
+                            rhs=words("rel", a, lo + at, P), rhs_scale=(picked["rel"], rel_sc1)[a][:, lo + at : lo + at + P],
+                            start=(a == 0 and i == first and at == 0), stop=False,
+                        )
+            for a in range(PASSES):
+                for i in range(first, first + slots):
                     cols = slice(i * P, (i + 1) * P)
                     nc.tensor.matmul_mx(
-                        out=t_ps[:, i, :], lhsT=wt_dw[:, a, 4 * i * P : 4 * (i + 1) * P].bitcast(E4M3), lhsT_scale=wt_ds[:, a, cols],
-                        rhs=words("tail", a, u), rhs_scale=picked["tail"][4 * a :, far],
-                        start=(a == 0 and i == 0), stop=(a == PASSES - 1 and i == PACK - 1),
-                    )
-            t_sb[u] = own([P, P, PACK], F32, tag or "t_sb%d" % u)
-            if u in TAIL_ON_VECTOR:
-                nc.vector.tensor_copy(out=t_sb[u][:], in_=t_ps[:].rearrange("p i j -> p j i"))
-            else:
-                nc.scalar.copy(out=t_sb[u][:], in_=t_ps[:].rearrange("p i j -> p j i"))
-
-        def project_a(u, bank):
-            far = slice(u * P, (u + 1) * P)
-            a_ps[u] = psum.tile([P, PACK, P], F32, name="a_ps", tag="bank%d" % bank)
-            for a in range(PASSES):
-                for i in range(PACK):
-                    nc.tensor.matmul_mx(
-                        out=a_ps[u][:, i, :], lhsT=wr_dw[:, a, 2 * i * P : 2 * (i + 1) * P].bitcast(E2M1), lhsT_scale=wr_ds[:, a, i * P : (i + 1) * P],
-                        rhs=words("rel", a, u), rhs_scale=(picked["rel"], rel_sc1)[a][:, far],
-                        start=(a == 0 and i == 0), stop=False,
-                    )
-            for a in range(PASSES):
-                for i in range(PACK):
-                    cols = slice(i * P, (i + 1) * P)
-                    nc.tensor.matmul_mx(
-                        out=a_ps[u][:, i, :], lhsT=wh_w[:, a, cols].bitcast(E4M3), lhsT_scale=wh_sc[:, a, cols],
-                        rhs=words("head", a, u), rhs_scale=picked["head"][4 * a :, far],
-                        start=False, stop=(a == PASSES - 1 and i == PACK - 1),
+                        out=a_ps[group, x][:, i - first, :], lhsT=wh_w[:, a, cols].bitcast(E4M3), lhsT_scale=wh_sc[:, a, cols],
+                        rhs=words("head", a, lo, n), rhs_scale=picked["head"][4 * a :, lo : lo + n],
+                        start=False, stop=(a == PASSES - 1 and i == first + slots - 1),
                     )
 
-        def subtract(u):
-            diff[u] = own([P, P, PACK], F32, "diff%d" % u)
-            woven = a_ps[u][:].rearrange("p i j -> p j i")
-            if u in SUB_ON_GPSIMD:
-                a_sb = own([P, P, PACK], F32, "a_sb%d" % u)
+        def subtract(group, x):
+            n, piece = len(group) * P, group[0] + x
+            slots = banks_of(group)[x][1]
+            diff[group, x] = own([P, n, slots], F32, "diff%d" % piece)
+            woven = a_ps[group, x][:].rearrange("p i j -> p j i")
+            if piece in SUB_ON_GPSIMD:
+                a_sb = own([P, n, slots], F32, "a_sb%d" % piece)
                 nc.scalar.copy(out=a_sb[:], in_=woven)
-                nc.gpsimd.tensor_tensor(out=diff[u][:], in0=a_sb[:], in1=t_sb[u][:], op=ALU.subtract)
+                nc.gpsimd.tensor_tensor(out=diff[group, x][:], in0=a_sb[:], in1=t_sb[group, x], op=ALU.subtract)
             else:
-                nc.vector.tensor_tensor(out=diff[u][:], in0=woven, in1=t_sb[u][:], op=ALU.subtract)
+                nc.vector.tensor_tensor(out=diff[group, x][:], in0=woven, in1=t_sb[group, x], op=ALU.subtract)
 
-        def exponential(u):
-            dist = own([P, P, PACK], F32, "dist%d" % u)
-            nc.scalar.activation(out=dist[:], in_=diff[u][:], func=ACT.Abs)
-            match[u] = own([P, P, PACK], F32, "match%d" % u)
-            nc.scalar.activation(out=match[u][:], in_=dist[:], func=ACT.Exp, scale=-1.0)
+        def exponential(group, x):
+            n, piece = len(group) * P, group[0] + x
+            slots = banks_of(group)[x][1]
+            dist = own([P, n, slots], F32, "dist%d" % piece)
+            nc.scalar.activation(out=dist[:], in_=diff[group, x][:], func=ACT.Abs)
+            if x == 0:
+                match[group] = own([P, len(group), n, slots], F32, "match%d" % piece)
+            nc.scalar.activation(out=match[group][:, x, :, :], in_=dist[:], func=ACT.Exp, scale=-1.0)
 
-        def weigh(u):
-            group = [gr for gr in GROUPS if u in gr][0]
-            if u == group[0]:
-                h_bf[group] = own([P, len(group) * P, PACK], BF16, "h_bf%d" % u)
-            at = (u - group[0]) * P
-            engine = nc.gpsimd if u in GAIN_ON_GPSIMD else nc.vector
-            engine.tensor_tensor(out=h_bf[group][:, at : at + P, :], in0=match[u][:], in1=gains[:].unsqueeze(1).to_broadcast([P, P, PACK]), op=ALU.mult)
+        def weigh(group):
+            n, parts = len(group) * P, len(group)
+            h_bf[group] = own([P, n, PACK], BF16, "h_bf%d" % group[0])
+            for u in group:
+                cols = slice((u - group[0]) * P, (u - group[0] + 1) * P)
+                engine = nc.gpsimd if u in GAIN_ON_GPSIMD else nc.vector
+                engine.tensor_tensor(
+                    out=h_bf[group][:, cols, :].rearrange("p j (x i) -> p j x i", x=parts),
+                    in0=match[group][:, :, cols, :].rearrange("p x j i -> p j x i"),
+                    in1=gains[:].rearrange("p (x i) -> p x i", x=parts).unsqueeze(1).to_broadcast([P, P, parts, PACK // parts]),
+                    op=ALU.mult,
+                )
 
         def quantise_h(group, tag=None):
             n = len(group) * P
@@ -254,76 +266,81 @@ def tile_list_triple_plausibility_readout_kernel(
         load_list("tail")
         load_tab(0)
         load_tab_scales()
-        load_tab(1)
         load_list("rel")
-        load_weight_scales(wt_sc, wt_scales)
-        load_wt()
+        load_tab(1)
         load_list("head")
         load_wh(0)
+        load_weight_scales(wt_sc, wt_scales)
+        load_wt()
         load_wh(1)
         gather([("tail", 0, 0, 2)], "tail0")
         gather_scales("tail")
-        gather([("tail", 1, 0, 1), ("tail", 1, 1, 1)], "tail1")
         gather_scales("rel")
         load_weight_scales(wr_sc, wr_scales)
         load_wr()
         lower_rel_scales()
         load_wo()
         load_bias()
+        gather([("tail", 1, 0, 2)], "tail1")
         gather_scales("head")
         gather([(n, a, 0, 1) for n in ("rel", "head") for a in (0, 1)], "first")
+        G = GROUPS
+        round_wh(0, PACK)
         wt_ds = deal(wt_sc, H, "wt_ds", nc.gpsimd)
         wt_dw = deal(wt_w, 4 * H, "wt_dw", nc.gpsimd)
-        project_tail(0, 0)
-        project_tail(1, 1)
-        round_wh(0, 0)
-        round_wh(1, 4)
-        project_tail(2, 2, "wh_raw1")
-        project_tail(3, 3, "wh_raw0")
+        round_wh(1, PACK)
+        early_t = own([P, 4, CHUNK, 2], F32, "wh_raw1")
+        project_tail(G[0], (0, 1), early_t)
+        project_tail(G[1], (2, 3), early_t)
         wr_ds = deal(wr_sc, H, "wr_ds", nc.gpsimd)
         wr_dw = deal(wr_w, 2 * H, "wr_dw", nc.gpsimd)
         quantise_wh(0)
         quantise_wh(1)
         LATE = [(n, a, c, 1) for n, c in (("rel", 1), ("head", 1), ("tail", 2), ("rel", 2), ("head", 2), ("tail", 3), ("rel", 3), ("head", 3)) for a in (0, 1)]
         gather(LATE[:16], "wh_bf1")
-        G = GROUPS
-        for u in range(4):
-            project_a(u, 4 + u)
-            subtract(u)
-            if u > 0:
-                exponential(u - 1)
-        round_wo(nc.gpsimd, "a_sb1")
-        project_tail(4, 4)
-        project_tail(5, 5)
-        exponential(3)
-        for u in range(4):
-            weigh(u)
-        project_a(4, 0)
-        subtract(4)
-        project_a(5, 1)
-        subtract(5)
+        for x in range(2):
+            project_a(G[0], x, 4 + x)
+            subtract(G[0], x)
 
-        project_tail(6, 6)
-        project_tail(7, 7)
-        exponential(4)
-        project_a(6, 2)
-        subtract(6)
-        exponential(5)
-        project_a(7, 3)
-        subtract(7)
-        exponential(6)
-        exponential(7)
+        project_a(G[1], 0, 0)
+        subtract(G[1], 0)
+        exponential(G[0], 0)
+        project_a(G[1], 1, 1)
+        subtract(G[1], 1)
+        exponential(G[0], 1)
+
+        project_tail(G[2], (4, 5))
+        weigh(G[0])
+        exponential(G[1], 0)
+        exponential(G[1], 1)
+        project_a(G[2], 0, 2)
+        subtract(G[2], 0)
+        project_a(G[2], 1, 3)
+        subtract(G[2], 1)
+
+        weigh(G[1])
+        project_tail(G[3], (0,))
+        project_tail(G[4], (1,))
+        exponential(G[2], 0)
+        exponential(G[2], 1)
+        project_a(G[3], 0, 4)
+        subtract(G[3], 0)
+        project_a(G[4], 0, 5)
+        subtract(G[4], 0)
+        exponential(G[3], 0)
+        exponential(G[4], 0)
+        round_wo(nc.vector, "t_sb4")
         quantise_wo("t_sb6")
         quantise_h(G[0], "t_sb7")
         quantise_h(G[1])
-        weigh(4)
-        weigh(5)
-        readout(G[0], 4)
+        weigh(G[2])
+        readout(G[0], 6)
         quantise_h(G[2])
-        weigh(6)
-        readout(G[1], 5)
+        weigh(G[3])
+        readout(G[1], 7)
         quantise_h(G[3])
-        weigh(7)
+        weigh(G[4])
         quantise_h(G[4])
-        for x in (2, 3, 4):
-            readout(G[x], x + 4 - 8 * (x // 4))
+        readout(G[2], 2)
+        readout(G[3], 3)
+        readout(G[4], 0)

@@ -27,6 +27,7 @@ BLOCKS = H // (PACK * RUN)
 GROUPS = [(0, 1), (2, 3), (4, 5), (6,), (7,)]
 SUB_ON_GPSIMD = (0, 1, 2, 3)
 GAIN_ON_GPSIMD = (0, 1, 2, 3)
+AFTER = {"a_sb3":"dist0","t_sb4":"dist1","t_sb5":"diff2","t_sb6":"dist2","t_sb7":"diff3"}
 BIAS_ON_SCALAR = (0, 2, 4, 6, 7)
 
 
@@ -48,15 +49,15 @@ def tile_list_triple_plausibility_readout_kernel(
         wr_w = keep.tile([P, PASSES, 2 * H], U8, name="wr_w", align_bytes=64)
         wh_w = keep.tile([P, PASSES, H], U32, name="wh_w", align_bytes=64)
         wh_sc = keep.tile([P, PASSES, H], U8, name="wh_sc", align_bytes=64)
-        wo_raw = keep.tile([P, PACK, N], F32, name="wo_raw")
+        wo_raw = keep.tile([P, PACK, N], F32, name="wo_raw", tag="wo_raw", align_bytes=64)
         gain = keep.tile([P, PACK, 8], F32, name="gain")
         gains = keep.tile([P, PACK], F32, name="gains")
         zero = keep.tile([P, PACK], F32, name="zero")
         bias = keep.tile([P, 2], F32, name="bias")
         out_v = out.rearrange("(c p) j -> p c j", c=2)
 
-        def own(shape, dtype, tag):
-            return keep.tile(shape, dtype, name=tag, tag=tag, align_bytes=64)
+        def own(shape, dtype, name):
+            return keep.tile(shape, dtype, name=name, tag=AFTER.get(name, name), align_bytes=64)
 
         def load_list(name):
             lists[name] = keep.tile([P, S // 16], U16, name="list_" + name)
@@ -76,9 +77,11 @@ def tile_list_triple_plausibility_readout_kernel(
                     in_=src[:, 4 * q : 4 * q + 4, :].rearrange("a r c -> r a c").bitcast(I32),
                 )
 
-        def load_tab(a):
-            tab[a] = keep.tile([P, T], I32, name="tab%d" % a, align_bytes=64)
-            nc.sync.dma_start(out=tab[a][:], in_=tab_words[a].rearrange("p t i -> p (t i)").bitcast(I32))
+        def load_tab():
+            both = keep.tile([P, PASSES, T], I32, name="tab", align_bytes=64)
+            nc.sync.dma_start(out=both[:], in_=tab_words.rearrange("a p t i -> p a (t i)").bitcast(I32))
+            for a in range(PASSES):
+                tab[a] = both[:, a, :]
 
         def load_wh(a):
             wh_raw[a] = own([P, PACK, H], F32, "wh_raw%d" % a)
@@ -99,7 +102,7 @@ def tile_list_triple_plausibility_readout_kernel(
             rows = g.rearrange("(q i e o) -> i q e o", i=PACK, e=RUN, o=1)
             with nc.allow_non_contiguous_dma(reason="one gain for each partition"):
                 for i in range(PACK):
-                    nc.scalar.dma_start(out=gain[:, i, 0:1], in_=rows[i])
+                    nc.sync.dma_start(out=gain[:, i, 0:1], in_=rows[i])
 
         def load_bias():
             with nc.allow_non_contiguous_dma(reason="two biases for each partition"):
@@ -135,17 +138,17 @@ def tile_list_triple_plausibility_readout_kernel(
             else:
                 nc.vector.tensor_copy(out=woven, in_=raw)
 
-        def quantise_wo(tag):
-            wo_q["w"] = own([P, N], U32, tag)
+        def quantise_wo(into):
+            wo_q["w"] = into
             wo_q["sc"] = own([P, N], U8, "wo_sc")
-            nc.vector.quantize_mx(out=wo_q["w"][:].bitcast(E4M3), scales=wo_q["sc"][:], in_=wo_q["bf"][:].rearrange("p n i -> p (n i)"))
+            nc.vector.quantize_mx(out=wo_q["w"].bitcast(E4M3), scales=wo_q["sc"][:], in_=wo_q["bf"][:].rearrange("p n i -> p (n i)"))
 
         def gather(jobs, tag):
             got = own([P, CHUNK * sum(job[3] for job in jobs)], U32, tag)
             at = 0
             for name, a, c0, n in jobs:
                 offsets = lists[name][:, c0 * CHUNK // 16 : (c0 + n) * CHUNK // 16]
-                nc.vector.tensor_copy(out=got[:, at : at + n * CHUNK], in_=tab[a][:].bitcast(U32).indirect(offsets))
+                nc.vector.tensor_copy(out=got[:, at : at + n * CHUNK], in_=tab[a].bitcast(U32).indirect(offsets))
                 for c in range(n):
                     picked[name, a, c0 + c] = got[:, at + c * CHUNK : at + (c + 1) * CHUNK]
                 at = at + n * CHUNK
@@ -164,21 +167,21 @@ def tile_list_triple_plausibility_readout_kernel(
         def words(name, a, lo, n):
             return picked[name, a, lo // CHUNK][:, lo % CHUNK : lo % CHUNK + n].bitcast(E4M3)
 
-        def project_tail(group, banks, shared=None):
+        def project_tail(group, x, bank, into=None):
             lo, n = group[0] * P, len(group) * P
-            for x, (first, slots) in enumerate(banks_of(group)):
-                t_ps = psum.tile([P, slots, n], F32, name="t_ps", tag="bank%d" % banks[x])
-                for a in range(PASSES):
-                    for i in range(first, first + slots):
-                        nc.tensor.matmul_mx(
-                            out=t_ps[:, i - first, :], lhsT=wt_dw[:, a, 4 * i * P : 4 * (i + 1) * P].bitcast(E4M3), lhsT_scale=wt_ds[:, a, i * P : (i + 1) * P],
-                            rhs=words("tail", a, lo, n), rhs_scale=picked["tail"][4 * a :, lo : lo + n],
-                            start=(a == 0 and i == first), stop=(a == PASSES - 1 and i == first + slots - 1),
-                        )
-                t_sb[group, x] = shared[:, group[0] + x, :, :] if shared is not None else own([P, n, slots], F32, "t_sb%d" % (group[0] + x))[:]
-                nc.scalar.copy(out=t_sb[group, x], in_=t_ps[:].rearrange("p i j -> p j i"))
+            first, slots = banks_of(group)[x]
+            t_ps = psum.tile([P, slots, n], F32, name="t_ps", tag="bank%d" % bank)
+            for a in range(PASSES):
+                for i in range(first, first + slots):
+                    nc.tensor.matmul_mx(
+                        out=t_ps[:, i - first, :], lhsT=wt_dw[:, a, 4 * i * P : 4 * (i + 1) * P].bitcast(E4M3), lhsT_scale=wt_ds[:, a, i * P : (i + 1) * P],
+                        rhs=words("tail", a, lo, n), rhs_scale=picked["tail"][4 * a :, lo : lo + n],
+                        start=(a == 0 and i == first), stop=(a == PASSES - 1 and i == first + slots - 1),
+                    )
+            t_sb[group, x] = into if into is not None else own([P, n, slots], F32, "t_sb%d" % (group[0] + x))[:]
+            nc.scalar.copy(out=t_sb[group, x], in_=t_ps[:].rearrange("p i j -> p j i"))
 
-        def project_a(group, x, bank):
+        def project_rel(group, x, bank):
             lo, n = group[0] * P, len(group) * P
             first, slots = banks_of(group)[x]
             a_ps[group, x] = psum.tile([P, slots, n], F32, name="a_ps", tag="bank%d" % bank)
@@ -190,7 +193,11 @@ def tile_list_triple_plausibility_readout_kernel(
                             rhs=words("rel", a, lo + at, P), rhs_scale=(picked["rel"], rel_sc1)[a][:, lo + at : lo + at + P],
                             start=(a == 0 and i == first and at == 0), stop=False,
                         )
-            for a in range(PASSES):
+
+        def project_head(group, x, passes):
+            lo, n = group[0] * P, len(group) * P
+            first, slots = banks_of(group)[x]
+            for a in passes:
                 for i in range(first, first + slots):
                     cols = slice(i * P, (i + 1) * P)
                     nc.tensor.matmul_mx(
@@ -199,23 +206,27 @@ def tile_list_triple_plausibility_readout_kernel(
                         start=False, stop=(a == PASSES - 1 and i == first + slots - 1),
                     )
 
-        def subtract(group, x):
+        def project_a(group, x, bank):
+            project_rel(group, x, bank)
+            project_head(group, x, range(PASSES))
+
+        def subtract(group, x, into=None):
             n, piece = len(group) * P, group[0] + x
             slots = banks_of(group)[x][1]
-            diff[group, x] = own([P, n, slots], F32, "diff%d" % piece)
+            diff[group, x] = into if into is not None else own([P, n, slots], F32, "diff%d" % piece)[:]
             woven = a_ps[group, x][:].rearrange("p i j -> p j i")
             if piece in SUB_ON_GPSIMD:
                 a_sb = own([P, n, slots], F32, "a_sb%d" % piece)
                 nc.scalar.copy(out=a_sb[:], in_=woven)
-                nc.gpsimd.tensor_tensor(out=diff[group, x][:], in0=a_sb[:], in1=t_sb[group, x], op=ALU.subtract)
+                nc.gpsimd.tensor_tensor(out=diff[group, x], in0=a_sb[:], in1=t_sb[group, x], op=ALU.subtract)
             else:
-                nc.vector.tensor_tensor(out=diff[group, x][:], in0=woven, in1=t_sb[group, x], op=ALU.subtract)
+                nc.vector.tensor_tensor(out=diff[group, x], in0=woven, in1=t_sb[group, x], op=ALU.subtract)
 
         def exponential(group, x):
             n, piece = len(group) * P, group[0] + x
             slots = banks_of(group)[x][1]
             dist = own([P, n, slots], F32, "dist%d" % piece)
-            nc.scalar.activation(out=dist[:], in_=diff[group, x][:], func=ACT.Abs)
+            nc.scalar.activation(out=dist[:], in_=diff[group, x], func=ACT.Abs)
             if x == 0:
                 match[group] = own([P, len(group), n, slots], F32, "match%d" % piece)
             nc.scalar.activation(out=match[group][:, x, :, :], in_=dist[:], func=ACT.Exp, scale=-1.0)
@@ -233,11 +244,11 @@ def tile_list_triple_plausibility_readout_kernel(
                     op=ALU.mult,
                 )
 
-        def quantise_h(group, tag=None):
+        def quantise_h(group, into=None):
             n = len(group) * P
-            h_w = own([P, n], U32, tag or "h_w%d" % group[0])
+            h_w = into if into is not None else own([P, n], U32, "h_w%d" % group[0])[:]
             h_sc = own([P, n], U8, "h_sc%d" % group[0])
-            nc.vector.quantize_mx(out=h_w[:].bitcast(E4M3), scales=h_sc[:], in_=h_bf[group][:].rearrange("p j i -> p (j i)"))
+            nc.vector.quantize_mx(out=h_w.bitcast(E4M3), scales=h_sc[:], in_=h_bf[group][:].rearrange("p j i -> p (j i)"))
             h_q[group] = (h_w, h_sc)
 
         def readout(group, bank):
@@ -248,7 +259,7 @@ def tile_list_triple_plausibility_readout_kernel(
                 nc.tensor.matmul_mx(
                     out=y_ps[:, c, :], lhsT=wo_q["w"][:, c * P : (c + 1) * P].bitcast(E4M3),
                     lhsT_scale=wo_q["sc"][:, c * P : (c + 1) * P],
-                    rhs=h_w[:].bitcast(E4M3), rhs_scale=h_sc[:], start=True, stop=True,
+                    rhs=h_w.bitcast(E4M3), rhs_scale=h_sc[:], start=True, stop=True,
                 )
             y_sb = own([P, 2, n], F32, "y_sb%d" % group[0])
             if group[0] in BIAS_ON_SCALAR:
@@ -258,17 +269,17 @@ def tile_list_triple_plausibility_readout_kernel(
                 nc.vector.tensor_tensor(out=y_sb[:], in0=y_ps[:], in1=bias[:].unsqueeze(2).to_broadcast([P, 2, n]), op=ALU.add)
             nc.sync.dma_start(out=out_v[:, :, group[0] * P : group[0] * P + n], in_=y_sb[:])
 
-        for plane in (tab_sc, wt_sc, wr_sc, rel_sc1):
+        nc.gpsimd.memset(tab_sc[:].bitcast(I32), 0)
+        for plane in (wt_sc, wr_sc, rel_sc1):
             nc.vector.memset(plane[:].bitcast(I32), 0)
-        load_gain()
         nc.vector.memset(zero[:], 0.0)
-        nc.gpsimd.tensor_tensor(out=gains[:], in0=gain[:, :, 0], in1=zero[:], op=ALU.add)
         load_list("tail")
-        load_tab(0)
-        load_tab_scales()
         load_list("rel")
-        load_tab(1)
         load_list("head")
+        load_tab_scales()
+        load_tab()
+        load_gain()
+        nc.gpsimd.tensor_tensor(out=gains[:], in0=gain[:, :, 0], in1=zero[:], op=ALU.add)
         load_wh(0)
         load_weight_scales(wt_sc, wt_scales)
         load_wt()
@@ -290,28 +301,29 @@ def tile_list_triple_plausibility_readout_kernel(
         wt_dw = deal(wt_w, 4 * H, "wt_dw", nc.gpsimd)
         round_wh(1, PACK)
         early_t = own([P, 4, CHUNK, 2], F32, "wh_raw1")
-        project_tail(G[0], (0, 1), early_t)
-        project_tail(G[1], (2, 3), early_t)
+        for piece in range(4):
+            project_tail(G[piece // 2], piece % 2, piece, early_t[:, piece, :, :])
         wr_ds = deal(wr_sc, H, "wr_ds", nc.gpsimd)
         wr_dw = deal(wr_w, 2 * H, "wr_dw", nc.gpsimd)
         quantise_wh(0)
         quantise_wh(1)
         LATE = [(n, a, c, 1) for n, c in (("rel", 1), ("head", 1), ("tail", 2), ("rel", 2), ("head", 2), ("tail", 3), ("rel", 3), ("head", 3)) for a in (0, 1)]
         gather(LATE[:16], "wh_bf1")
-        for x in range(2):
-            project_a(G[0], x, 4 + x)
-            subtract(G[0], x)
-
+        project_a(G[0], 0, 4)
+        subtract(G[0], 0)
+        project_a(G[0], 1, 5)
+        subtract(G[0], 1)
+        round_wo(nc.scalar, "wo_bf")
         project_a(G[1], 0, 0)
-        subtract(G[1], 0)
-        exponential(G[0], 0)
         project_a(G[1], 1, 1)
-        subtract(G[1], 1)
+        exponential(G[0], 0)
+        subtract(G[1], 0)
         exponential(G[0], 1)
-
-        project_tail(G[2], (4, 5))
+        subtract(G[1], 1)
+        project_tail(G[2], 0, 4)
         weigh(G[0])
         exponential(G[1], 0)
+        project_tail(G[2], 1, 5)
         exponential(G[1], 1)
         project_a(G[2], 0, 2)
         subtract(G[2], 0)
@@ -319,28 +331,31 @@ def tile_list_triple_plausibility_readout_kernel(
         subtract(G[2], 1)
 
         weigh(G[1])
-        project_tail(G[3], (0,))
-        project_tail(G[4], (1,))
+        project_tail(G[3], 0, 6)
+        project_tail(G[4], 0, 7)
         exponential(G[2], 0)
         exponential(G[2], 1)
-        project_a(G[3], 0, 4)
+        project_rel(G[3], 0, 0)
+        project_rel(G[4], 0, 1)
+        for a in range(PASSES):
+            project_head(G[3], 0, (a,))
+            project_head(G[4], 0, (a,))
         subtract(G[3], 0)
-        project_a(G[4], 0, 5)
         subtract(G[4], 0)
         exponential(G[3], 0)
         exponential(G[4], 0)
-        round_wo(nc.vector, "t_sb4")
-        quantise_wo("t_sb6")
-        quantise_h(G[0], "t_sb7")
-        quantise_h(G[1])
+        late_words = own([P, 3 * CHUNK], U32, "diff3")
+        quantise_wo(late_words[:, :N])
+        quantise_h(G[0], late_words[:, CHUNK : 2 * CHUNK])
+        quantise_h(G[1], late_words[:, 2 * CHUNK :])
         weigh(G[2])
-        readout(G[0], 6)
+        readout(G[0], 4)
         quantise_h(G[2])
         weigh(G[3])
-        readout(G[1], 7)
+        readout(G[1], 5)
         quantise_h(G[3])
         weigh(G[4])
         quantise_h(G[4])
         readout(G[2], 2)
         readout(G[3], 3)
-        readout(G[4], 0)
+        readout(G[4], 6)

@@ -25,10 +25,14 @@ TILES = S // P
 RUN = 8
 BLOCKS = H // (PACK * RUN)
 GROUPS = [(0, 1), (2, 3), (4, 5), (6,), (7,)]
-SUB_ON_GPSIMD = (0, 1, 2, 3)
-GAIN_ON_GPSIMD = (0, 1, 2, 3)
-AFTER = {"a_sb3":"dist0","t_sb4":"dist1","t_sb5":"diff2","t_sb6":"dist2","t_sb7":"diff3"}
+C2_ON_G = 0
+GAINS_ON_G = 4
+AFTER = {"late":"wr_w","wt_ds":"wh_bf0","wt_dw":"wh_bf1","late_words":"t_sb6"}
 BIAS_ON_SCALAR = (0, 2, 4, 6, 7)
+
+
+def WO_ENGINE(nc):
+    return nc.scalar
 
 
 def tile_list_triple_plausibility_readout_kernel(
@@ -40,18 +44,19 @@ def tile_list_triple_plausibility_readout_kernel(
         psum = ctx.enter_context(tc.psum_pool(name="psum", bufs=1))
 
         lists, picked, wh_raw, wh_bf, tab = {}, {}, {}, {}, {}
-        t_sb, a_ps, diff, match, h_bf, h_q, wo_q = {}, {}, {}, {}, {}, {}, {}
+        t_ps, t_sb, a_ps, a_sb, diff, dist, match, h_bf, h_q, wo_q = {}, {}, {}, {}, {}, {}, {}, {}, {}, {}
         tab_sc = keep.tile([P, T], U8, name="tab_sc", align_bytes=64)
-        wt_sc = keep.tile([P, PASSES, H], U8, name="wt_sc", align_bytes=64)
-        wr_sc = keep.tile([P, PASSES, H], U8, name="wr_sc", align_bytes=64)
+        wt_sc = keep.tile([P, PASSES, H], U8, name="wt_sc", tag="wt_sc", align_bytes=64)
+        wr_sc = keep.tile([P, PASSES, H], U8, name="wr_sc", tag="wr_sc", align_bytes=64)
         rel_sc1 = keep.tile([P, S], U8, name="rel_sc1", align_bytes=64)
-        wt_w = keep.tile([P, PASSES, 4 * H], U8, name="wt_w", align_bytes=64)
-        wr_w = keep.tile([P, PASSES, 2 * H], U8, name="wr_w", align_bytes=64)
+        wt_w = keep.tile([P, PASSES, 4 * H], U8, name="wt_w", tag="wt_w", align_bytes=64)
+        wr_w = keep.tile([P, PASSES, 2 * H], U8, name="wr_w", tag="wr_w", align_bytes=64)
         wh_w = keep.tile([P, PASSES, H], U32, name="wh_w", align_bytes=64)
         wh_sc = keep.tile([P, PASSES, H], U8, name="wh_sc", align_bytes=64)
         wo_raw = keep.tile([P, PACK, N], F32, name="wo_raw", tag="wo_raw", align_bytes=64)
         gain = keep.tile([P, PACK, 8], F32, name="gain")
-        gains = keep.tile([P, PACK], F32, name="gains")
+        gain4 = keep.tile([P, PACK], F32, name="gain4")
+        gains = keep.tile([P, P, PACK], F32, name="gains")
         zero = keep.tile([P, PACK], F32, name="zero")
         bias = keep.tile([P, 2], F32, name="bias")
         out_v = out.rearrange("(c p) j -> p c j", c=2)
@@ -77,11 +82,10 @@ def tile_list_triple_plausibility_readout_kernel(
                     in_=src[:, 4 * q : 4 * q + 4, :].rearrange("a r c -> r a c").bitcast(I32),
                 )
 
-        def load_tab():
-            both = keep.tile([P, PASSES, T], I32, name="tab", align_bytes=64)
-            nc.sync.dma_start(out=both[:], in_=tab_words.rearrange("a p t i -> p a (t i)").bitcast(I32))
-            for a in range(PASSES):
-                tab[a] = both[:, a, :]
+        def load_tab(a):
+            half = keep.tile([P, T], I32, name="tab%d" % a, align_bytes=64)
+            nc.sync.dma_start(out=half[:], in_=tab_words[a].rearrange("p t i -> p (t i)").bitcast(I32))
+            tab[a] = half[:]
 
         def load_wh(a):
             wh_raw[a] = own([P, PACK, H], F32, "wh_raw%d" % a)
@@ -109,7 +113,7 @@ def tile_list_triple_plausibility_readout_kernel(
                 nc.sync.dma_start(out=bias[:], in_=b.rearrange("(c p) -> p c", c=2))
 
         def deal(src, width, name, engine):
-            dealt = keep.tile([P, PASSES, width], U8, name=name, align_bytes=64)
+            dealt = own([P, PASSES, width], U8, name)
             engine.tensor_copy(
                 out=dealt[:].bitcast(I32).rearrange("p a (i q e) -> p a i q e", i=PACK, q=BLOCKS),
                 in_=src[:].bitcast(I32).rearrange("p a (q i e) -> p a i q e", i=PACK, q=BLOCKS),
@@ -160,6 +164,11 @@ def tile_list_triple_plausibility_readout_kernel(
         def lower_rel_scales():
             nc.sync.dma_start(out=rel_sc1[0:100, :].bitcast(I32), in_=picked["rel"][4:104, :].bitcast(I32))
 
+        def plane(name, a, lo, n):
+            if name == "rel":
+                return (picked[name], rel_sc1)[a][:, lo : lo + n]
+            return picked[name][4 * a :, lo : lo + n]
+
         def banks_of(group):
             slots = PACK // len(group)
             return [(first, slots) for first in range(0, PACK, slots)]
@@ -167,82 +176,63 @@ def tile_list_triple_plausibility_readout_kernel(
         def words(name, a, lo, n):
             return picked[name, a, lo // CHUNK][:, lo % CHUNK : lo % CHUNK + n].bitcast(E4M3)
 
-        def project_tail(group, x, bank, into=None):
+        def project(name, group, x, a, bank=None, last=False):
             lo, n = group[0] * P, len(group) * P
             first, slots = banks_of(group)[x]
-            t_ps = psum.tile([P, slots, n], F32, name="t_ps", tag="bank%d" % bank)
-            for a in range(PASSES):
-                for i in range(first, first + slots):
+            sums = t_ps if name == "tail" else a_ps
+            if bank is not None:
+                sums[group, x] = psum.tile([P, slots, n], F32, name="sum_%s%d" % (name, group[0] + x), tag="bank%d" % bank)
+            width = P if name == "rel" else n
+            for i in range(first, first + slots):
+                for at in range(0, n, width):
+                    if name == "tail":
+                        w, w_sc = wt_dw[:, a, 4 * i * P : 4 * (i + 1) * P].bitcast(E4M3), wt_ds[:, a, i * P : (i + 1) * P]
+                    elif name == "rel":
+                        w, w_sc = wr_dw[:, a, 2 * i * P : 2 * (i + 1) * P].bitcast(E2M1), wr_ds[:, a, i * P : (i + 1) * P]
+                    else:
+                        w, w_sc = wh_w[:, a, i * P : (i + 1) * P].bitcast(E4M3), wh_sc[:, a, i * P : (i + 1) * P]
                     nc.tensor.matmul_mx(
-                        out=t_ps[:, i - first, :], lhsT=wt_dw[:, a, 4 * i * P : 4 * (i + 1) * P].bitcast(E4M3), lhsT_scale=wt_ds[:, a, i * P : (i + 1) * P],
-                        rhs=words("tail", a, lo, n), rhs_scale=picked["tail"][4 * a :, lo : lo + n],
-                        start=(a == 0 and i == first), stop=(a == PASSES - 1 and i == first + slots - 1),
-                    )
-            t_sb[group, x] = into if into is not None else own([P, n, slots], F32, "t_sb%d" % (group[0] + x))[:]
-            nc.scalar.copy(out=t_sb[group, x], in_=t_ps[:].rearrange("p i j -> p j i"))
-
-        def project_rel(group, x, bank):
-            lo, n = group[0] * P, len(group) * P
-            first, slots = banks_of(group)[x]
-            a_ps[group, x] = psum.tile([P, slots, n], F32, name="a_ps", tag="bank%d" % bank)
-            for a in range(PASSES):
-                for i in range(first, first + slots):
-                    for at in range(0, n, P):
-                        nc.tensor.matmul_mx(
-                            out=a_ps[group, x][:, i - first, at : at + P], lhsT=wr_dw[:, a, 2 * i * P : 2 * (i + 1) * P].bitcast(E2M1), lhsT_scale=wr_ds[:, a, i * P : (i + 1) * P],
-                            rhs=words("rel", a, lo + at, P), rhs_scale=(picked["rel"], rel_sc1)[a][:, lo + at : lo + at + P],
-                            start=(a == 0 and i == first and at == 0), stop=False,
-                        )
-
-        def project_head(group, x, passes):
-            lo, n = group[0] * P, len(group) * P
-            first, slots = banks_of(group)[x]
-            for a in passes:
-                for i in range(first, first + slots):
-                    cols = slice(i * P, (i + 1) * P)
-                    nc.tensor.matmul_mx(
-                        out=a_ps[group, x][:, i - first, :], lhsT=wh_w[:, a, cols].bitcast(E4M3), lhsT_scale=wh_sc[:, a, cols],
-                        rhs=words("head", a, lo, n), rhs_scale=picked["head"][4 * a :, lo : lo + n],
-                        start=False, stop=(a == PASSES - 1 and i == first + slots - 1),
+                        out=sums[group, x][:, i - first, at : at + width], lhsT=w, lhsT_scale=w_sc,
+                        rhs=words(name, a, lo + at, width), rhs_scale=plane(name, a, lo + at, width),
+                        start=(bank is not None and i == first and at == 0), stop=(last and i == first + slots - 1 and at + width == n),
                     )
 
-        def project_a(group, x, bank):
-            project_rel(group, x, bank)
-            project_head(group, x, range(PASSES))
+        def empty_t(group, x):
+            n, slots = len(group) * P, banks_of(group)[x][1]
+            t_sb[group, x] = own([P, n, slots], F32, "t_sb%d" % (group[0] + x))
+            nc.scalar.copy(out=t_sb[group, x][:], in_=t_ps[group, x][:].rearrange("p i j -> p j i"))
 
-        def subtract(group, x, into=None):
-            n, piece = len(group) * P, group[0] + x
-            slots = banks_of(group)[x][1]
-            diff[group, x] = into if into is not None else own([P, n, slots], F32, "diff%d" % piece)[:]
-            woven = a_ps[group, x][:].rearrange("p i j -> p j i")
-            if piece in SUB_ON_GPSIMD:
-                a_sb = own([P, n, slots], F32, "a_sb%d" % piece)
-                nc.scalar.copy(out=a_sb[:], in_=woven)
-                nc.gpsimd.tensor_tensor(out=diff[group, x], in0=a_sb[:], in1=t_sb[group, x], op=ALU.subtract)
+        def empty_a(group, x):
+            n, slots = len(group) * P, banks_of(group)[x][1]
+            a_sb[group, x] = own([P, n, slots], F32, "a_sb%d" % (group[0] + x))
+            nc.scalar.copy(out=a_sb[group, x][:], in_=a_ps[group, x][:].rearrange("p i j -> p j i"))
+
+        def subtract(group, x):
+            n, slots = len(group) * P, banks_of(group)[x][1]
+            diff[group, x] = own([P, n, slots], F32, "diff%d" % (group[0] + x))
+            if (group, x) in a_sb:
+                nc.gpsimd.tensor_tensor(out=diff[group, x][:], in0=a_sb[group, x][:], in1=t_sb[group, x][:], op=ALU.subtract)
             else:
-                nc.vector.tensor_tensor(out=diff[group, x], in0=woven, in1=t_sb[group, x], op=ALU.subtract)
+                nc.vector.tensor_tensor(out=diff[group, x][:], in0=a_ps[group, x][:].rearrange("p i j -> p j i"), in1=t_sb[group, x][:], op=ALU.subtract)
 
-        def exponential(group, x):
-            n, piece = len(group) * P, group[0] + x
-            slots = banks_of(group)[x][1]
-            dist = own([P, n, slots], F32, "dist%d" % piece)
-            nc.scalar.activation(out=dist[:], in_=diff[group, x], func=ACT.Abs)
+        def absolute(group, x):
+            n, slots = len(group) * P, banks_of(group)[x][1]
             if x == 0:
-                match[group] = own([P, len(group), n, slots], F32, "match%d" % piece)
-            nc.scalar.activation(out=match[group][:, x, :, :], in_=dist[:], func=ACT.Exp, scale=-1.0)
+                dist[group] = own([P, len(group), n, slots], F32, "dist%d" % group[0])
+            nc.scalar.activation(out=dist[group][:, x, :, :], in_=diff[group, x][:], func=ACT.Abs)
 
-        def weigh(group):
-            n, parts = len(group) * P, len(group)
-            h_bf[group] = own([P, n, PACK], BF16, "h_bf%d" % group[0])
-            for u in group:
-                cols = slice((u - group[0]) * P, (u - group[0] + 1) * P)
-                engine = nc.gpsimd if u in GAIN_ON_GPSIMD else nc.vector
-                engine.tensor_tensor(
-                    out=h_bf[group][:, cols, :].rearrange("p j (x i) -> p j x i", x=parts),
-                    in0=match[group][:, :, cols, :].rearrange("p x j i -> p j x i"),
-                    in1=gains[:].rearrange("p (x i) -> p x i", x=parts).unsqueeze(1).to_broadcast([P, P, parts, PACK // parts]),
-                    op=ALU.mult,
-                )
+        def exponential(group, u):
+            cols = slice((u - group[0]) * P, (u - group[0] + 1) * P)
+            match[u] = own([P, P, PACK], F32, "match%d" % u)
+            nc.scalar.activation(
+                out=match[u][:].rearrange("p j (x i) -> p j x i", x=len(group)),
+                in_=dist[group][:, :, cols, :].rearrange("p x j i -> p j x i"), func=ACT.Exp, scale=-1.0,
+            )
+
+        def weigh(group, u, engine):
+            if u == group[0]:
+                h_bf[group] = own([P, len(group) * P, PACK], BF16, "h_bf%d" % group[0])
+            engine.tensor_tensor(out=h_bf[group][:, (u - group[0]) * P : (u - group[0] + 1) * P, :], in0=match[u][:], in1=gains[:], op=ALU.mult)
 
         def quantise_h(group, into=None):
             n = len(group) * P
@@ -270,92 +260,130 @@ def tile_list_triple_plausibility_readout_kernel(
             nc.sync.dma_start(out=out_v[:, :, group[0] * P : group[0] * P + n], in_=y_sb[:])
 
         nc.gpsimd.memset(tab_sc[:].bitcast(I32), 0)
-        for plane in (wt_sc, wr_sc, rel_sc1):
-            nc.vector.memset(plane[:].bitcast(I32), 0)
+        for zeroed in (wt_sc, wr_sc, rel_sc1):
+            nc.vector.memset(zeroed[:].bitcast(I32), 0)
         nc.vector.memset(zero[:], 0.0)
         load_list("tail")
-        load_list("rel")
         load_list("head")
+        load_list("rel")
         load_tab_scales()
-        load_tab()
-        load_gain()
-        nc.gpsimd.tensor_tensor(out=gains[:], in0=gain[:, :, 0], in1=zero[:], op=ALU.add)
         load_wh(0)
+        load_wh(1)
+        load_gain()
+        nc.gpsimd.tensor_tensor(out=gain4[:], in0=gain[:, :, 0], in1=zero[:], op=ALU.add)
+        load_tab(0)
         load_weight_scales(wt_sc, wt_scales)
         load_wt()
-        load_wh(1)
-        gather([("tail", 0, 0, 2)], "tail0")
+        load_tab(1)
         gather_scales("tail")
+        gather_scales("head")
         gather_scales("rel")
         load_weight_scales(wr_sc, wr_scales)
         load_wr()
         lower_rel_scales()
         load_wo()
         load_bias()
-        gather([("tail", 1, 0, 2)], "tail1")
-        gather_scales("head")
-        gather([(n, a, 0, 1) for n in ("rel", "head") for a in (0, 1)], "first")
         G = GROUPS
         round_wh(0, PACK)
-        wt_ds = deal(wt_sc, H, "wt_ds", nc.gpsimd)
-        wt_dw = deal(wt_w, 4 * H, "wt_dw", nc.gpsimd)
         round_wh(1, PACK)
-        early_t = own([P, 4, CHUNK, 2], F32, "wh_raw1")
-        for piece in range(4):
-            project_tail(G[piece // 2], piece % 2, piece, early_t[:, piece, :, :])
-        wr_ds = deal(wr_sc, H, "wr_ds", nc.gpsimd)
-        wr_dw = deal(wr_w, 2 * H, "wr_dw", nc.gpsimd)
+        nc.scalar.copy(out=gains[:], in_=gain4[:].unsqueeze(1).to_broadcast([P, P, PACK]))
         quantise_wh(0)
         quantise_wh(1)
-        LATE = [(n, a, c, 1) for n, c in (("rel", 1), ("head", 1), ("tail", 2), ("rel", 2), ("head", 2), ("tail", 3), ("rel", 3), ("head", 3)) for a in (0, 1)]
-        gather(LATE[:16], "wh_bf1")
-        project_a(G[0], 0, 4)
-        subtract(G[0], 0)
-        project_a(G[0], 1, 5)
-        subtract(G[0], 1)
-        round_wo(nc.scalar, "wo_bf")
-        project_a(G[1], 0, 0)
-        project_a(G[1], 1, 1)
-        exponential(G[0], 0)
+        wt_ds = deal(wt_sc, H, "wt_ds", nc.gpsimd)
+        wt_dw = deal(wt_w, 4 * H, "wt_dw", nc.gpsimd)
+        wr_ds = deal(wr_sc, H, "wr_ds", nc.gpsimd)
+        wr_dw = deal(wr_w, 2 * H, "wr_dw", nc.gpsimd)
+        gather([("head", 0, 0, 1), ("tail", 0, 0, 1), ("rel", 0, 0, 1)], "early0")
+        gather([("tail", 1, 0, 1), ("head", 1, 0, 1), ("rel", 1, 0, 1)], "early1")
+        gather([(n, a, c, 1) for c in (1, 2, 3) for n in ("tail", "rel", "head") for a in (0, 1)], "late")
+        for x in range(2):
+            project("head", G[0], x, 0, bank=4 + x)
+        for x in range(2):
+            project("tail", G[0], x, 0, bank=x)
+        for x in range(2):
+            project("tail", G[0], x, 1, last=True)
+            empty_t(G[0], x)
+        for x in range(2):
+            project("head", G[0], x, 1)
+        for x in range(2):
+            project("rel", G[0], x, 0)
+            project("rel", G[0], x, 1, last=True)
+            empty_a(G[0], x)
+            subtract(G[0], x)
+        for x in range(2):
+            project("tail", G[1], x, 0, bank=2 + x)
+            project("tail", G[1], x, 1, last=True)
+            empty_t(G[1], x)
+        round_wo(WO_ENGINE(nc), "wo_bf")
+        for x in range(2):
+            project("rel", G[1], x, 0, bank=6 + x)
+            project("rel", G[1], x, 1)
+        for x in range(2):
+            project("head", G[1], x, 0)
+            project("head", G[1], x, 1, last=True)
+        absolute(G[0], 0)
+        empty_a(G[1], 0)
         subtract(G[1], 0)
-        exponential(G[0], 1)
+        absolute(G[0], 1)
+        empty_a(G[1], 1)
         subtract(G[1], 1)
-        project_tail(G[2], 0, 4)
-        weigh(G[0])
-        exponential(G[1], 0)
-        project_tail(G[2], 1, 5)
-        exponential(G[1], 1)
-        project_a(G[2], 0, 2)
-        subtract(G[2], 0)
-        project_a(G[2], 1, 3)
-        subtract(G[2], 1)
-
-        weigh(G[1])
-        project_tail(G[3], 0, 6)
-        project_tail(G[4], 0, 7)
-        exponential(G[2], 0)
-        exponential(G[2], 1)
-        project_rel(G[3], 0, 0)
-        project_rel(G[4], 0, 1)
+        for u in G[0]:
+            exponential(G[0], u)
+            weigh(G[0], u, nc.gpsimd)
+        for x in range(2):
+            project("tail", G[2], x, 0, bank=x)
+            project("tail", G[2], x, 1, last=True)
+        for x in range(2):
+            project("rel", G[2], x, 0, bank=2 + x)
+            project("rel", G[2], x, 1)
+        for x in range(2):
+            project("head", G[2], x, 0)
+            project("head", G[2], x, 1, last=True)
+        for x in range(2):
+            absolute(G[1], x)
+            empty_t(G[2], x)
+        for x in range(2):
+            exponential(G[1], G[1][x])
+            if x < C2_ON_G:
+                empty_a(G[2], x)
+                subtract(G[2], x)
+        for u in G[1]:
+            weigh(G[1], u, nc.gpsimd if u < GAINS_ON_G else nc.vector)
+        for k in (3, 4):
+            project("tail", G[k], 0, 0, bank=k + 1)
+            project("tail", G[k], 0, 1, last=True)
+            empty_t(G[k], 0)
+        for x in range(C2_ON_G, 2):
+            subtract(G[2], x)
+        for x in range(2):
+            absolute(G[2], x)
+        for u in G[2]:
+            exponential(G[2], u)
+        for k in (3, 4):
+            project("rel", G[k], 0, 0, bank=k + 3)
+            project("rel", G[k], 0, 1)
         for a in range(PASSES):
-            project_head(G[3], 0, (a,))
-            project_head(G[4], 0, (a,))
-        subtract(G[3], 0)
-        subtract(G[4], 0)
-        exponential(G[3], 0)
-        exponential(G[4], 0)
-        late_words = own([P, 3 * CHUNK], U32, "diff3")
+            for k in (3, 4):
+                project("head", G[k], 0, a, last=(a == 1))
+        for k in (3, 4):
+            subtract(G[k], 0)
+        for k in (3, 4):
+            absolute(G[k], 0)
+        for k in (3, 4):
+            exponential(G[k], G[k][0])
+        late_words = own([P, 3 * CHUNK], U32, "late_words")
         quantise_wo(late_words[:, :N])
         quantise_h(G[0], late_words[:, CHUNK : 2 * CHUNK])
         quantise_h(G[1], late_words[:, 2 * CHUNK :])
-        weigh(G[2])
-        readout(G[0], 4)
+        for u in G[2]:
+            weigh(G[2], u, nc.vector)
+        weigh(G[3], 6, nc.vector)
         quantise_h(G[2])
-        weigh(G[3])
-        readout(G[1], 5)
+        weigh(G[4], 7, nc.vector)
         quantise_h(G[3])
-        weigh(G[4])
         quantise_h(G[4])
+        readout(G[0], 0)
+        readout(G[1], 1)
         readout(G[2], 2)
         readout(G[3], 3)
-        readout(G[4], 6)
+        readout(G[4], 4)

@@ -83,7 +83,7 @@ def tile_list_triple_plausibility_readout_kernel(
                 )
 
         def load_tab(a):
-            half = keep.tile([P, T], I32, name="tab%d" % a, align_bytes=64)
+            half = own([P, T], I32, "tab%d" % a)
             nc.sync.dma_start(out=half[:], in_=tab_words[a].rearrange("p t i -> p (t i)").bitcast(I32))
             tab[a] = half[:]
 
@@ -295,7 +295,12 @@ def tile_list_triple_plausibility_readout_kernel(
         wr_dw = deal(wr_w, 2 * H, "wr_dw", nc.gpsimd)
         gather([("head", 0, 0, 1), ("tail", 0, 0, 1), ("rel", 0, 0, 1)], "early0")
         gather([("tail", 1, 0, 1), ("head", 1, 0, 1), ("rel", 1, 0, 1)], "early1")
-        gather([(n, a, c, 1) for c in (1, 2, 3) for n in ("tail", "rel", "head") for a in (0, 1)], "late")
+        gather(
+            [(n, a, 1, 1) for n in ("tail", "rel", "head") for a in (0, 1)]
+            + [("tail", 0, 2, 2), ("tail", 1, 2, 2), ("rel", 0, 2, 2), ("head", 0, 2, 2)]
+            + [(n, 1, c, 1) for c in (2, 3) for n in ("rel", "head")],
+            "late",
+        )
         for x in range(2):
             project("head", G[0], x, 0, bank=4 + x)
         for x in range(2):
@@ -332,39 +337,37 @@ def tile_list_triple_plausibility_readout_kernel(
             weigh(G[0], u, nc.gpsimd)
         for x in range(2):
             project("tail", G[2], x, 0, bank=x)
+        for k in (3, 4):
+            project("tail", G[k], 0, 0, bank=k - 1)
+        for x in range(2):
             project("tail", G[2], x, 1, last=True)
-        for x in range(2):
-            project("rel", G[2], x, 0, bank=2 + x)
-            project("rel", G[2], x, 1)
-        for x in range(2):
-            project("head", G[2], x, 0)
-            project("head", G[2], x, 1, last=True)
+        for k in (3, 4):
+            project("tail", G[k], 0, 1, last=True)
         for x in range(2):
             absolute(G[1], x)
             empty_t(G[2], x)
-        for x in range(2):
-            exponential(G[1], G[1][x])
-            if x < C2_ON_G:
-                empty_a(G[2], x)
-                subtract(G[2], x)
         for u in G[1]:
-            weigh(G[1], u, nc.gpsimd if u < GAINS_ON_G else nc.vector)
+            exponential(G[1], u)
+            weigh(G[1], u, nc.gpsimd)
         for k in (3, 4):
-            project("tail", G[k], 0, 0, bank=k + 1)
-            project("tail", G[k], 0, 1, last=True)
             empty_t(G[k], 0)
-        for x in range(C2_ON_G, 2):
+        for name, a in (("rel", 0), ("head", 0)):
+            for x in range(2):
+                project(name, G[2], x, a, bank=(4 + x if (name, a) == ("rel", 0) else None))
+            for k in (3, 4):
+                project(name, G[k], 0, a, bank=(k + 3 if (name, a) == ("rel", 0) else None))
+        for x in range(2):
+            project("rel", G[2], x, 1)
+        for x in range(2):
+            project("head", G[2], x, 1, last=True)
             subtract(G[2], x)
+        for name in ("rel", "head"):
+            for k in (3, 4):
+                project(name, G[k], 0, 1, last=(name == "head"))
         for x in range(2):
             absolute(G[2], x)
         for u in G[2]:
             exponential(G[2], u)
-        for k in (3, 4):
-            project("rel", G[k], 0, 0, bank=k + 3)
-            project("rel", G[k], 0, 1)
-        for a in range(PASSES):
-            for k in (3, 4):
-                project("head", G[k], 0, a, last=(a == 1))
         for k in (3, 4):
             subtract(G[k], 0)
         for k in (3, 4):

@@ -28,7 +28,8 @@ GROUPS = [(0, 1), (2, 3), (4, 5), (6,), (7,)]
 C2_ON_G = 0
 GAINS_ON_G = 4
 AFTER = {"late":"wr_w","wt_ds":"wh_bf0","wt_dw":"wh_bf1","late_words":"t_sb6"}
-BIAS_ON_SCALAR = (0, 2, 4, 6, 7)
+ABS_ON_VECTOR = (7,)
+BIAS_ON_SCALAR = (0, 2, 4, 6)
 
 
 def WO_ENGINE(nc):
@@ -209,17 +210,22 @@ def tile_list_triple_plausibility_readout_kernel(
 
         def subtract(group, x):
             n, slots = len(group) * P, banks_of(group)[x][1]
-            diff[group, x] = own([P, n, slots], F32, "diff%d" % (group[0] + x))
+            if x == 0:
+                diff[group] = own([P, len(group), n, slots], F32, "diff%d" % group[0])
             if (group, x) in a_sb:
-                nc.gpsimd.tensor_tensor(out=diff[group, x][:], in0=a_sb[group, x][:], in1=t_sb[group, x][:], op=ALU.subtract)
+                nc.gpsimd.tensor_tensor(out=diff[group][:, x, :, :], in0=a_sb[group, x][:], in1=t_sb[group, x][:], op=ALU.subtract)
             else:
-                nc.vector.tensor_tensor(out=diff[group, x][:], in0=a_ps[group, x][:].rearrange("p i j -> p j i"), in1=t_sb[group, x][:], op=ALU.subtract)
+                nc.vector.tensor_tensor(out=diff[group][:, x, :, :], in0=a_ps[group, x][:].rearrange("p i j -> p j i"), in1=t_sb[group, x][:], op=ALU.subtract)
 
         def absolute(group, x):
             n, slots = len(group) * P, banks_of(group)[x][1]
             if x == 0:
                 dist[group] = own([P, len(group), n, slots], F32, "dist%d" % group[0])
-            nc.scalar.activation(out=dist[group][:, x, :, :], in_=diff[group, x][:], func=ACT.Abs)
+            if group[0] in ABS_ON_VECTOR:
+                d = diff[group][:, x, :, :]
+                nc.vector.scalar_tensor_tensor(out=dist[group][:, x, :, :], in0=d, scalar=-1.0, in1=d, op0=ALU.mult, op1=ALU.max)
+            else:
+                nc.scalar.activation(out=dist[group][:, x, :, :], in_=diff[group][:, x, :, :], func=ACT.Abs)
 
         def exponential(group, u):
             cols = slice((u - group[0]) * P, (u - group[0] + 1) * P)

@@ -27,7 +27,7 @@ BLOCKS = H // (PACK * RUN)
 GROUPS = [(0, 1), (2, 3), (4, 5), (6,), (7,)]
 C2_ON_G = 0
 GAINS_ON_G = 4
-AFTER = {"late":"wr_w","wt_ds":"wh_bf0","wt_dw":"wh_bf1","late_words":"t_sb6"}
+AFTER = {"late":"wr_w","late_words":"t_sb6"}
 ABS_ON_VECTOR = (7,)
 BIAS_ON_SCALAR = (0, 2, 4, 6)
 
@@ -115,9 +115,11 @@ def tile_list_triple_plausibility_readout_kernel(
 
         def deal(src, width, name, engine):
             dealt = own([P, PASSES, width], U8, name)
-            engine.tensor_copy(
-                out=dealt[:].bitcast(I32).rearrange("p a (i q e) -> p a i q e", i=PACK, q=BLOCKS),
-                in_=src[:].bitcast(I32).rearrange("p a (q i e) -> p a i q e", i=PACK, q=BLOCKS),
+            move = engine.copy if engine is nc.scalar else engine.tensor_copy
+            view = U32 if engine is nc.scalar else I32
+            move(
+                out=dealt[:].bitcast(view).rearrange("p a (i q e) -> p a i q e", i=PACK, q=BLOCKS),
+                in_=src[:].bitcast(view).rearrange("p a (q i e) -> p a i q e", i=PACK, q=BLOCKS),
             )
             return dealt
 
@@ -292,11 +294,11 @@ def tile_list_triple_plausibility_readout_kernel(
         G = GROUPS
         round_wh(0, PACK)
         round_wh(1, PACK)
-        nc.scalar.copy(out=gains[:], in_=gain4[:].unsqueeze(1).to_broadcast([P, P, PACK]))
         quantise_wh(0)
         quantise_wh(1)
-        wt_ds = deal(wt_sc, H, "wt_ds", nc.gpsimd)
-        wt_dw = deal(wt_w, 4 * H, "wt_dw", nc.gpsimd)
+        wt_ds = deal(wt_sc, H, "wt_ds", nc.scalar)
+        wt_dw = deal(wt_w, 4 * H, "wt_dw", nc.scalar)
+        nc.scalar.copy(out=gains[:], in_=gain4[:].unsqueeze(1).to_broadcast([P, P, PACK]))
         wr_ds = deal(wr_sc, H, "wr_ds", nc.gpsimd)
         wr_dw = deal(wr_w, 2 * H, "wr_dw", nc.gpsimd)
         gather([("head", 0, 0, 1), ("tail", 0, 0, 1), ("rel", 0, 0, 1)], "early0")

@@ -27,7 +27,7 @@ BLOCKS = H // (PACK * RUN)
 GROUPS = [(0, 1), (2, 3), (4, 5), (6,), (7,)]
 C2_ON_G = 0
 GAINS_ON_G = 4
-AFTER = {"late":"wr_w","late_words":"t_sb6"}
+AFTER = {"wh_sc1":"wt_sc","late":"wr_w","late_words":"t_sb6"}
 ABS_ON_VECTOR = (7,)
 BIAS_ON_SCALAR = (0, 2, 4, 6)
 
@@ -53,7 +53,7 @@ def tile_list_triple_plausibility_readout_kernel(
         wt_w = keep.tile([P, PASSES, 4 * H], U8, name="wt_w", tag="wt_w", align_bytes=64)
         wr_w = keep.tile([P, PASSES, 2 * H], U8, name="wr_w", tag="wr_w", align_bytes=64)
         wh_w = keep.tile([P, PASSES, H], U32, name="wh_w", align_bytes=64)
-        wh_sc = keep.tile([P, PASSES, H], U8, name="wh_sc", align_bytes=64)
+        wh_sc = {}
         wo_raw = keep.tile([P, PACK, N], F32, name="wo_raw", tag="wo_raw", align_bytes=64)
         gain = keep.tile([P, PACK, 8], F32, name="gain")
         gain4 = keep.tile([P, PACK], F32, name="gain4")
@@ -70,11 +70,17 @@ def tile_list_triple_plausibility_readout_kernel(
             nc.sync.dma_start(lists[name][:], {"head": offs, "rel": offs2, "tail": offs3}[name])
 
         def load_tab_scales():
-            for q in range(4):
+            for q in range(2):
                 nc.sync.dma_start(
                     out=tab_sc[32 * q : 32 * q + 8, :].bitcast(I32),
                     in_=tab_scales[:, 4 * q : 4 * q + 4, :].bitcast(I32),
                 )
+            for q in range(2, 4):
+                for a in range(PASSES):
+                    nc.sync.dma_start(
+                        out=tab_sc[32 * q + 4 * a : 32 * q + 4 * a + 4, :].bitcast(I32),
+                        in_=tab_scales[a, 4 * q : 4 * q + 4, :].bitcast(I32),
+                    )
 
         def load_weight_scales(sc, src):
             for q in range(4):
@@ -127,12 +133,17 @@ def tile_list_triple_plausibility_readout_kernel(
             wh_bf[a] = own([P, PACK, BLOCKS, RUN, PACK], BF16, "wh_bf%d" % a)
             raw = wh_raw[a][:].rearrange("p k (q i e) -> p i q e k", i=PACK, e=RUN)
             if on_scalar:
-                nc.scalar.copy(out=wh_bf[a][:, :on_scalar, :, :, :], in_=raw[:, :on_scalar, :, :, :])
+                for i in range(on_scalar):
+                    nc.scalar.copy(
+                        out=wh_bf[a][:, i, :, :, :].rearrange("p q (h e) k -> p q h k e", h=2),
+                        in_=raw[:, i, :, :, :].rearrange("p q (h e) k -> p q h k e", h=2),
+                    )
             for i in range(on_scalar, PACK):
                 nc.gpsimd.tensor_scalar(out=wh_bf[a][:, i, :, :, :], in0=raw[:, i, :, :, :], scalar1=1.0, scalar2=0.0, op0=ALU.mult, op1=ALU.add)
 
         def quantise_wh(a):
-            nc.vector.quantize_mx(out=wh_w[:, a, :].bitcast(E4M3), scales=wh_sc[:, a, :], in_=wh_bf[a][:].rearrange("p i q e k -> p (i q e k)"))
+            wh_sc[a] = own([P, H], U8, "wh_sc%d" % a)
+            nc.vector.quantize_mx(out=wh_w[:, a, :].bitcast(E4M3), scales=wh_sc[a][:], in_=wh_bf[a][:].rearrange("p i q e k -> p (i q e k)"))
 
         def round_wo(engine, tag):
             wo_q["bf"] = own([P, N, PACK], BF16, tag)
@@ -185,7 +196,7 @@ def tile_list_triple_plausibility_readout_kernel(
             sums = t_ps if name == "tail" else a_ps
             if bank is not None:
                 sums[group, x] = psum.tile([P, slots, n], F32, name="sum_%s%d" % (name, group[0] + x), tag="bank%d" % bank)
-            width = P if name == "rel" else n
+            width = n
             for i in range(first, first + slots):
                 for at in range(0, n, width):
                     if name == "tail":
@@ -193,7 +204,7 @@ def tile_list_triple_plausibility_readout_kernel(
                     elif name == "rel":
                         w, w_sc = wr_dw[:, a, 2 * i * P : 2 * (i + 1) * P].bitcast(E2M1), wr_ds[:, a, i * P : (i + 1) * P]
                     else:
-                        w, w_sc = wh_w[:, a, i * P : (i + 1) * P].bitcast(E4M3), wh_sc[:, a, i * P : (i + 1) * P]
+                        w, w_sc = wh_w[:, a, i * P : (i + 1) * P].bitcast(E4M3), wh_sc[a][:, i * P : (i + 1) * P]
                     nc.tensor.matmul_mx(
                         out=sums[group, x][:, i - first, at : at + width], lhsT=w, lhsT_scale=w_sc,
                         rhs=words(name, a, lo + at, width), rhs_scale=plane(name, a, lo + at, width),
@@ -273,9 +284,9 @@ def tile_list_triple_plausibility_readout_kernel(
         nc.vector.memset(zero[:], 0.0)
         load_list("tail")
         load_list("head")
-        load_list("rel")
         load_tab_scales()
         load_wh(0)
+        load_list("rel")
         load_wh(1)
         load_gain()
         nc.gpsimd.tensor_tensor(out=gain4[:], in0=gain[:, :, 0], in1=zero[:], op=ALU.add)
@@ -295,24 +306,25 @@ def tile_list_triple_plausibility_readout_kernel(
         round_wh(0, PACK)
         round_wh(1, PACK)
         quantise_wh(0)
-        quantise_wh(1)
         wt_ds = deal(wt_sc, H, "wt_ds", nc.scalar)
         wt_dw = deal(wt_w, 4 * H, "wt_dw", nc.scalar)
         nc.scalar.copy(out=gains[:], in_=gain4[:].unsqueeze(1).to_broadcast([P, P, PACK]))
         wr_ds = deal(wr_sc, H, "wr_ds", nc.gpsimd)
         wr_dw = deal(wr_w, 2 * H, "wr_dw", nc.gpsimd)
-        gather([("head", 0, 0, 1), ("tail", 0, 0, 1), ("rel", 0, 0, 1)], "early0")
+        gather([("head", 0, 0, 1), ("tail", 0, 0, 2), ("rel", 0, 0, 1)], "early0")
+        quantise_wh(1)
         gather([("tail", 1, 0, 1), ("head", 1, 0, 1), ("rel", 1, 0, 1)], "early1")
         gather(
-            [(n, a, 1, 1) for n in ("tail", "rel", "head") for a in (0, 1)]
+            [("tail", 1, 1, 1)] + [(n, a, 1, 1) for n in ("rel", "head") for a in (0, 1)]
             + [("tail", 0, 2, 2), ("tail", 1, 2, 2), ("rel", 0, 2, 2), ("head", 0, 2, 2)]
             + [(n, 1, c, 1) for c in (2, 3) for n in ("rel", "head")],
             "late",
         )
         for x in range(2):
             project("head", G[0], x, 0, bank=4 + x)
-        for x in range(2):
-            project("tail", G[0], x, 0, bank=x)
+        for k in range(2):
+            for x in range(2):
+                project("tail", G[k], x, 0, bank=2 * k + x)
         for x in range(2):
             project("tail", G[0], x, 1, last=True)
             empty_t(G[0], x)
@@ -324,7 +336,6 @@ def tile_list_triple_plausibility_readout_kernel(
             empty_a(G[0], x)
             subtract(G[0], x)
         for x in range(2):
-            project("tail", G[1], x, 0, bank=2 + x)
             project("tail", G[1], x, 1, last=True)
             empty_t(G[1], x)
         round_wo(WO_ENGINE(nc), "wo_bf")

from contextlib import ExitStack

import concourse.mybir as mybir

K, H, N, T, S = 1024, 512, 256, 2048, 1024
FLOPS = 2 * (3 * K * H * S + H * N * S)

F32 = mybir.dt.float32
BF16 = mybir.dt.bfloat16
I32 = mybir.dt.int32
U32 = mybir.dt.uint32
U16 = mybir.dt.uint16
U8 = mybir.dt.uint8
E4M3 = mybir.dt.float8_e4m3fn_x4
E2M1 = mybir.dt.float4_e2m1fn_x4
ACT = mybir.ActivationFunctionType
ALU = mybir.AluOpType

P = 128
PACK = 4
PASSES = K // (P * PACK)
CHUNK = 256
CHUNKS = S // CHUNK
TILES = S // P
RUN = 8
BLOCKS = H // (PACK * RUN)
GROUPS = [(0, 1), (2, 3), (4, 5), (6,), (7,)]
C2_ON_G = 0
GAINS_ON_G = 4
AFTER = {"wh_sc1":"wt_sc","late":"wr_w","late_words":"t_sb6"}
ABS_ON_VECTOR = (7,)
BIAS_ON_SCALAR = (0, 2, 4, 6)


def WO_ENGINE(nc):
    return nc.scalar


def tile_list_triple_plausibility_readout_kernel(
    tc, tab_words, tab_scales, offs, offs2, offs3, wh, wr_words, wr_scales, wt_words, wt_scales, g, wo, b, out
):
    nc = tc.nc
    with ExitStack() as ctx:
        keep = ctx.enter_context(tc.tile_pool(name="keep", bufs=1))
        psum = ctx.enter_context(tc.psum_pool(name="psum", bufs=1))

        lists, picked, wh_raw, wh_bf, tab = {}, {}, {}, {}, {}
        t_ps, t_sb, a_ps, a_sb, diff, dist, match, h_bf, h_q, wo_q = {}, {}, {}, {}, {}, {}, {}, {}, {}, {}
        tab_sc = keep.tile([P, T], U8, name="tab_sc", align_bytes=64)
        wt_sc = keep.tile([P, PASSES, H], U8, name="wt_sc", tag="wt_sc", align_bytes=64)
        wr_sc = keep.tile([P, PASSES, H], U8, name="wr_sc", tag="wr_sc", align_bytes=64)
        rel_sc1 = keep.tile([P, S], U8, name="rel_sc1", align_bytes=64)
        wt_w = keep.tile([P, PASSES, 4 * H], U8, name="wt_w", tag="wt_w", align_bytes=64)
        wr_w = keep.tile([P, PASSES, 2 * H], U8, name="wr_w", tag="wr_w", align_bytes=64)
        wh_w = keep.tile([P, PASSES, H], U32, name="wh_w", align_bytes=64)
        wh_sc = {}
        wo_raw = keep.tile([P, PACK, N], F32, name="wo_raw", tag="wo_raw", align_bytes=64)
        gain = keep.tile([P, PACK, 8], F32, name="gain")
        gain4 = keep.tile([P, PACK], F32, name="gain4")
        gains = keep.tile([P, P, PACK], F32, name="gains")
        zero = keep.tile([P, PACK], F32, name="zero")
        bias = keep.tile([P, 2], F32, name="bias")
        out_v = out.rearrange("(c p) j -> p c j", c=2)

        def own(shape, dtype, name):
            return keep.tile(shape, dtype, name=name, tag=AFTER.get(name, name), align_bytes=64)

        def load_list(name):
            lists[name] = keep.tile([P, S // 16], U16, name="list_" + name)
            nc.sync.dma_start(lists[name][:], {"head": offs, "rel": offs2, "tail": offs3}[name])

        def load_tab_scales():
            for q in range(2):
                nc.sync.dma_start(
                    out=tab_sc[32 * q : 32 * q + 8, :].bitcast(I32),
                    in_=tab_scales[:, 4 * q : 4 * q + 4, :].bitcast(I32),
                )
            for q in range(2, 4):
                for a in range(PASSES):
                    nc.sync.dma_start(
                        out=tab_sc[32 * q + 4 * a : 32 * q + 4 * a + 4, :].bitcast(I32),
                        in_=tab_scales[a, 4 * q : 4 * q + 4, :].bitcast(I32),
                    )

        def load_weight_scales(sc, src):
            for q in range(4):
                nc.sync.dma_start(
                    out=sc[32 * q : 32 * q + 4, :, :].bitcast(I32),
                    in_=src[:, 4 * q : 4 * q + 4, :].rearrange("a r c -> r a c").bitcast(I32),
                )

        def load_tab(a):
            half = own([P, T], I32, "tab%d" % a)
            nc.sync.dma_start(out=half[:], in_=tab_words[a].rearrange("p t i -> p (t i)").bitcast(I32))
            tab[a] = half[:]

        def load_wh(a):
            wh_raw[a] = own([P, PACK, H], F32, "wh_raw%d" % a)
            nc.sync.dma_start(out=wh_raw[a][:], in_=wh[512 * a : 512 * (a + 1), :].rearrange("(p i) c -> p i c", i=PACK))

        def load_wt():
            nc.sync.dma_start(out=wt_w[:].bitcast(I32), in_=wt_words.rearrange("a p c i -> p a (c i)").bitcast(I32))

        def load_wr():
            nc.sync.dma_start(out=wr_w[:].bitcast(I32), in_=wr_words.rearrange("a p c -> p a c").bitcast(I32))

        def load_wo():
            rows = wo.rearrange("(q i e) n -> i q e n", i=PACK, e=RUN)
            for i in range(PACK):
                nc.sync.dma_start(out=wo_raw[:, i, :], in_=rows[i])

        def load_gain():
            rows = g.rearrange("(q i e o) -> i q e o", i=PACK, e=RUN, o=1)
            with nc.allow_non_contiguous_dma(reason="one gain for each partition"):
                for i in range(PACK):
                    nc.sync.dma_start(out=gain[:, i, 0:1], in_=rows[i])

        def load_bias():
            with nc.allow_non_contiguous_dma(reason="two biases for each partition"):
                nc.sync.dma_start(out=bias[:], in_=b.rearrange("(c p) -> p c", c=2))

        def deal(src, width, name, engine):
            dealt = own([P, PASSES, width], U8, name)
            move = engine.copy if engine is nc.scalar else engine.tensor_copy
            view = U32 if engine is nc.scalar else I32
            move(
                out=dealt[:].bitcast(view).rearrange("p a (i q e) -> p a i q e", i=PACK, q=BLOCKS),
                in_=src[:].bitcast(view).rearrange("p a (q i e) -> p a i q e", i=PACK, q=BLOCKS),
            )
            return dealt

        def round_wh(a, on_scalar):
            wh_bf[a] = own([P, PACK, BLOCKS, RUN, PACK], BF16, "wh_bf%d" % a)
            raw = wh_raw[a][:].rearrange("p k (q i e) -> p i q e k", i=PACK, e=RUN)
            if on_scalar:
                for i in range(on_scalar):
                    nc.scalar.copy(
                        out=wh_bf[a][:, i, :, :, :].rearrange("p q (h e) k -> p q h k e", h=2),
                        in_=raw[:, i, :, :, :].rearrange("p q (h e) k -> p q h k e", h=2),
                    )
            for i in range(on_scalar, PACK):
                nc.gpsimd.tensor_scalar(out=wh_bf[a][:, i, :, :, :], in0=raw[:, i, :, :, :], scalar1=1.0, scalar2=0.0, op0=ALU.mult, op1=ALU.add)

        def quantise_wh(a):
            wh_sc[a] = own([P, H], U8, "wh_sc%d" % a)
            nc.vector.quantize_mx(out=wh_w[:, a, :].bitcast(E4M3), scales=wh_sc[a][:], in_=wh_bf[a][:].rearrange("p i q e k -> p (i q e k)"))

        def round_wo(engine, tag):
            wo_q["bf"] = own([P, N, PACK], BF16, tag)
            woven = wo_q["bf"][:].rearrange("p (c d) i -> p c i d", d=4)
            raw = wo_raw[:].rearrange("p i (c d) -> p c i d", d=4)
            if engine is nc.gpsimd:
                nc.gpsimd.tensor_scalar(out=woven, in0=raw, scalar1=1.0, scalar2=0.0, op0=ALU.mult, op1=ALU.add)
            elif engine is nc.scalar:
                nc.scalar.copy(out=woven, in_=raw)
            else:
                nc.vector.tensor_copy(out=woven, in_=raw)

        def quantise_wo(into):
            wo_q["w"] = into
            wo_q["sc"] = own([P, N], U8, "wo_sc")
            nc.vector.quantize_mx(out=wo_q["w"].bitcast(E4M3), scales=wo_q["sc"][:], in_=wo_q["bf"][:].rearrange("p n i -> p (n i)"))

        def gather(jobs, tag):
            got = own([P, CHUNK * sum(job[3] for job in jobs)], U32, tag)
            at = 0
            for name, a, c0, n in jobs:
                offsets = lists[name][:, c0 * CHUNK // 16 : (c0 + n) * CHUNK // 16]
                nc.vector.tensor_copy(out=got[:, at : at + n * CHUNK], in_=tab[a].bitcast(U32).indirect(offsets))
                for c in range(n):
                    picked[name, a, c0 + c] = got[:, at + c * CHUNK : at + (c + 1) * CHUNK]
                at = at + n * CHUNK

        def gather_scales(name):
            picked[name] = own([P, S], U8, "sc_" + name)
            nc.vector.tensor_copy(out=picked[name][:], in_=tab_sc[:].indirect(lists[name][:]))

        def lower_rel_scales():
            nc.sync.dma_start(out=rel_sc1[0:100, :].bitcast(I32), in_=picked["rel"][4:104, :].bitcast(I32))

        def plane(name, a, lo, n):
            if name == "rel":
                return (picked[name], rel_sc1)[a][:, lo : lo + n]
            return picked[name][4 * a :, lo : lo + n]

        def banks_of(group):
            slots = PACK // len(group)
            return [(first, slots) for first in range(0, PACK, slots)]

        def words(name, a, lo, n):
            return picked[name, a, lo // CHUNK][:, lo % CHUNK : lo % CHUNK + n].bitcast(E4M3)

        def project(name, group, x, a, bank=None, last=False):
            lo, n = group[0] * P, len(group) * P
            first, slots = banks_of(group)[x]
            sums = t_ps if name == "tail" else a_ps
            if bank is not None:
                sums[group, x] = psum.tile([P, slots, n], F32, name="sum_%s%d" % (name, group[0] + x), tag="bank%d" % bank)
            width = n
            for i in range(first, first + slots):
                for at in range(0, n, width):
                    if name == "tail":
                        w, w_sc = wt_dw[:, a, 4 * i * P : 4 * (i + 1) * P].bitcast(E4M3), wt_ds[:, a, i * P : (i + 1) * P]
                    elif name == "rel":
                        w, w_sc = wr_dw[:, a, 2 * i * P : 2 * (i + 1) * P].bitcast(E2M1), wr_ds[:, a, i * P : (i + 1) * P]
                    else:
                        w, w_sc = wh_w[:, a, i * P : (i + 1) * P].bitcast(E4M3), wh_sc[a][:, i * P : (i + 1) * P]
                    nc.tensor.matmul_mx(
                        out=sums[group, x][:, i - first, at : at + width], lhsT=w, lhsT_scale=w_sc,
                        rhs=words(name, a, lo + at, width), rhs_scale=plane(name, a, lo + at, width),
                        start=(bank is not None and i == first and at == 0), stop=(last and i == first + slots - 1 and at + width == n),
                    )

        def empty_t(group, x):
            n, slots = len(group) * P, banks_of(group)[x][1]
            t_sb[group, x] = own([P, n, slots], F32, "t_sb%d" % (group[0] + x))
            nc.scalar.copy(out=t_sb[group, x][:], in_=t_ps[group, x][:].rearrange("p i j -> p j i"))

        def empty_a(group, x):
            n, slots = len(group) * P, banks_of(group)[x][1]
            a_sb[group, x] = own([P, n, slots], F32, "a_sb%d" % (group[0] + x))
            nc.scalar.copy(out=a_sb[group, x][:], in_=a_ps[group, x][:].rearrange("p i j -> p j i"))

        def subtract(group, x):
            n, slots = len(group) * P, banks_of(group)[x][1]
            if x == 0:
                diff[group] = own([P, len(group), n, slots], F32, "diff%d" % group[0])
            if (group, x) in a_sb:
                nc.gpsimd.tensor_tensor(out=diff[group][:, x, :, :], in0=a_sb[group, x][:], in1=t_sb[group, x][:], op=ALU.subtract)
            else:
                nc.vector.tensor_tensor(out=diff[group][:, x, :, :], in0=a_ps[group, x][:].rearrange("p i j -> p j i"), in1=t_sb[group, x][:], op=ALU.subtract)

        def absolute(group, x):
            n, slots = len(group) * P, banks_of(group)[x][1]
            if x == 0:
                dist[group] = own([P, len(group), n, slots], F32, "dist%d" % group[0])
            if group[0] in ABS_ON_VECTOR:
                d = diff[group][:, x, :, :]
                nc.vector.scalar_tensor_tensor(out=dist[group][:, x, :, :], in0=d, scalar=-1.0, in1=d, op0=ALU.mult, op1=ALU.max)
            else:
                nc.scalar.activation(out=dist[group][:, x, :, :], in_=diff[group][:, x, :, :], func=ACT.Abs)

        def exponential(group, u):
            cols = slice((u - group[0]) * P, (u - group[0] + 1) * P)
            match[u] = own([P, P, PACK], F32, "match%d" % u)
            nc.scalar.activation(
                out=match[u][:].rearrange("p j (x i) -> p j x i", x=len(group)),
                in_=dist[group][:, :, cols, :].rearrange("p x j i -> p j x i"), func=ACT.Exp, scale=-1.0,
            )

        def weigh(group, u, engine):
            if u == group[0]:
                h_bf[group] = own([P, len(group) * P, PACK], BF16, "h_bf%d" % group[0])
            engine.tensor_tensor(out=h_bf[group][:, (u - group[0]) * P : (u - group[0] + 1) * P, :], in0=match[u][:], in1=gains[:], op=ALU.mult)

        def quantise_h(group, into=None):
            n = len(group) * P
            h_w = into if into is not None else own([P, n], U32, "h_w%d" % group[0])[:]
            h_sc = own([P, n], U8, "h_sc%d" % group[0])
            nc.vector.quantize_mx(out=h_w.bitcast(E4M3), scales=h_sc[:], in_=h_bf[group][:].rearrange("p j i -> p (j i)"))
            h_q[group] = (h_w, h_sc)

        def readout(group, bank):
            n = len(group) * P
            h_w, h_sc = h_q[group]
            y_ps = psum.tile([P, 2, n], F32, name="y_ps", tag="bank%d" % bank)
            for c in range(2):
                nc.tensor.matmul_mx(
                    out=y_ps[:, c, :], lhsT=wo_q["w"][:, c * P : (c + 1) * P].bitcast(E4M3),
                    lhsT_scale=wo_q["sc"][:, c * P : (c + 1) * P],
                    rhs=h_w.bitcast(E4M3), rhs_scale=h_sc[:], start=True, stop=True,
                )
            y_sb = own([P, 2, n], F32, "y_sb%d" % group[0])
            if group[0] in BIAS_ON_SCALAR:
                for c in range(2):
                    nc.scalar.activation(out=y_sb[:, c, :], in_=y_ps[:, c, :], func=ACT.Identity, bias=bias[:, c : c + 1])
            else:
                nc.vector.tensor_tensor(out=y_sb[:], in0=y_ps[:], in1=bias[:].unsqueeze(2).to_broadcast([P, 2, n]), op=ALU.add)
            nc.sync.dma_start(out=out_v[:, :, group[0] * P : group[0] * P + n], in_=y_sb[:])

        nc.gpsimd.memset(tab_sc[:].bitcast(I32), 0)
        for zeroed in (wt_sc, wr_sc, rel_sc1):
            nc.vector.memset(zeroed[:].bitcast(I32), 0)
        nc.vector.memset(zero[:], 0.0)
        load_list("tail")
        load_list("head")
        load_tab_scales()
        load_wh(0)
        load_list("rel")
        load_wh(1)
        load_gain()
        nc.gpsimd.tensor_tensor(out=gain4[:], in0=gain[:, :, 0], in1=zero[:], op=ALU.add)
        load_tab(0)
        load_weight_scales(wt_sc, wt_scales)
        load_wt()
        load_tab(1)
        gather_scales("tail")
        gather_scales("head")
        gather_scales("rel")
        load_weight_scales(wr_sc, wr_scales)
        load_wr()
        lower_rel_scales()
        load_wo()
        load_bias()
        G = GROUPS
        round_wh(0, PACK)
        round_wh(1, PACK)
        quantise_wh(0)
        wt_ds = deal(wt_sc, H, "wt_ds", nc.scalar)
        wt_dw = deal(wt_w, 4 * H, "wt_dw", nc.scalar)
        nc.scalar.copy(out=gains[:], in_=gain4[:].unsqueeze(1).to_broadcast([P, P, PACK]))
        wr_ds = deal(wr_sc, H, "wr_ds", nc.gpsimd)
        wr_dw = deal(wr_w, 2 * H, "wr_dw", nc.gpsimd)
        gather([("head", 0, 0, 1), ("tail", 0, 0, 2), ("rel", 0, 0, 1)], "early0")
        quantise_wh(1)
        gather([("tail", 1, 0, 1), ("head", 1, 0, 1), ("rel", 1, 0, 1)], "early1")
        gather(
            [("tail", 1, 1, 1)] + [(n, a, 1, 1) for n in ("rel", "head") for a in (0, 1)]
            + [("tail", 0, 2, 2), ("tail", 1, 2, 2), ("rel", 0, 2, 2), ("head", 0, 2, 2)]
            + [(n, 1, c, 1) for c in (2, 3) for n in ("rel", "head")],
            "late",
        )
        for x in range(2):
            project("head", G[0], x, 0, bank=4 + x)
        for k in range(2):
            for x in range(2):
                project("tail", G[k], x, 0, bank=2 * k + x)
        for x in range(2):
            project("tail", G[0], x, 1, last=True)
            empty_t(G[0], x)
        for x in range(2):
            project("head", G[0], x, 1)
        for x in range(2):
            project("rel", G[0], x, 0)
            project("rel", G[0], x, 1, last=True)
            empty_a(G[0], x)
            subtract(G[0], x)
        for x in range(2):
            project("tail", G[1], x, 1, last=True)
            empty_t(G[1], x)
        round_wo(WO_ENGINE(nc), "wo_bf")
        for x in range(2):
            project("rel", G[1], x, 0, bank=6 + x)
            project("rel", G[1], x, 1)
        for x in range(2):
            project("head", G[1], x, 0)
            project("head", G[1], x, 1, last=True)
        absolute(G[0], 0)
        empty_a(G[1], 0)
        subtract(G[1], 0)
        absolute(G[0], 1)
        empty_a(G[1], 1)
        subtract(G[1], 1)
        for u in G[0]:
            exponential(G[0], u)
            weigh(G[0], u, nc.gpsimd)
        for x in range(2):
            project("tail", G[2], x, 0, bank=x)
        for k in (3, 4):
            project("tail", G[k], 0, 0, bank=k - 1)
        for x in range(2):
            project("tail", G[2], x, 1, last=True)
        for k in (3, 4):
            project("tail", G[k], 0, 1, last=True)
        for x in range(2):
            absolute(G[1], x)
            empty_t(G[2], x)
        for u in G[1]:
            exponential(G[1], u)
            weigh(G[1], u, nc.gpsimd)
        for k in (3, 4):
            empty_t(G[k], 0)
        for name, a in (("rel", 0), ("head", 0)):
            for x in range(2):
                project(name, G[2], x, a, bank=(4 + x if (name, a) == ("rel", 0) else None))
            for k in (3, 4):
                project(name, G[k], 0, a, bank=(k + 3 if (name, a) == ("rel", 0) else None))
        for x in range(2):
            project("rel", G[2], x, 1)
        for x in range(2):
            project("head", G[2], x, 1, last=True)
            subtract(G[2], x)
        for name in ("rel", "head"):
            for k in (3, 4):
                project(name, G[k], 0, 1, last=(name == "head"))
        for x in range(2):
            absolute(G[2], x)
        for u in G[2]:
            exponential(G[2], u)
        for k in (3, 4):
            subtract(G[k], 0)
        for k in (3, 4):
            absolute(G[k], 0)
        for k in (3, 4):
            exponential(G[k], G[k][0])
        late_words = own([P, 3 * CHUNK], U32, "late_words")
        quantise_wo(late_words[:, :N])
        quantise_h(G[0], late_words[:, CHUNK : 2 * CHUNK])
        quantise_h(G[1], late_words[:, 2 * CHUNK :])
        for u in G[2]:
            weigh(G[2], u, nc.vector)
        weigh(G[3], 6, nc.vector)
        quantise_h(G[2])
        weigh(G[4], 7, nc.vector)
        quantise_h(G[3])
        quantise_h(G[4])
        readout(G[0], 0)
        readout(G[1], 1)
        readout(G[2], 2)
        readout(G[3], 3)
        readout(G[4], 4)
